import numpy as np
import ml_dtypes


def mxq(x, axis, fmt="e4m3"):
    dtype, down = {"e4m3": (ml_dtypes.float8_e4m3fn, 7), "e5m2": (ml_dtypes.float8_e5m2, 14)}[fmt]
    v = np.moveaxis(np.asarray(x, np.float32).astype(ml_dtypes.bfloat16).astype(np.float64), axis, -1)
    blocks = v.reshape(v.shape[:-1] + (-1, 32))
    amax = np.abs(blocks).max(-1, keepdims=True)
    byte = np.maximum(np.where(amax > 0, np.frexp(amax)[1] - 1 + 127, 0) - down, 1)
    scale = np.exp2(byte - 127.0)
    codes = (blocks / scale).astype(np.float32).astype(dtype).astype(np.float64)
    return np.moveaxis((codes * scale).reshape(v.shape), -1, axis)


WIDE = False


def mx_kscale(k):
    if not WIDE:
        return np.ones(k)
    levels = np.array([10, -10, 5, -5, 0])
    if k % 512:
        return np.exp2(np.random.permutation(np.resize(levels, k // 32))).repeat(32)
    a = np.empty((k // 512, 16))
    for p in range(k // 512):
        a[p, :8] = np.random.permutation(np.resize(levels, 8))
        for g in range(8):
            far = levels[np.abs(levels - a[p, g]) >= 10]
            a[p, g + 8] = far[np.random.randint(len(far))]
    return np.exp2(a.ravel()).repeat(32)


def f64(x):
    return np.asarray(x).astype(np.float64)


def striped(idx):
    return np.tile(idx.reshape(-1, 16).T, (8, 1)).astype(np.uint16)


def unstriped(offs):
    return offs[:16].T.reshape(-1).astype(np.int64)


def pack_weight(w):
    k, n = w.shape
    w = f64(np.asarray(w, np.float32).astype(ml_dtypes.bfloat16)).reshape(k // 32, 32, n)
    amax = np.abs(w).max(1)
    byte = np.clip(np.where(amax > 0, np.frexp(amax)[1] - 1 + 127 - 7, 1), 1, 254)
    scaled = (w * np.exp2(127.0 - byte)[:, None, :]).reshape(k, n).astype(np.float32)
    words = np.ascontiguousarray(scaled.reshape(k // 512, 128, 4, n).transpose(0, 1, 3, 2)).astype(ml_dtypes.float8_e4m3fn).view(np.uint8)
    return words, np.ascontiguousarray(byte.astype(np.uint8).reshape(k // 512, 16, n))


def unpack_weight(words, scales):
    g, p, n, _ = words.shape
    vals = np.ascontiguousarray(words).view(ml_dtypes.float8_e4m3fn).astype(np.float64) * np.repeat(np.exp2(scales.astype(np.float64) - 127.0), 8, axis=1)[..., None]
    return vals.transpose(0, 1, 3, 2).reshape(g * 512, n)


K, T, S, J = 512, 1024, 512, 512
P = 2 ** 7


def setup_inputs():
    n = np.random.standard_normal
    s = mx_kscale(K)[:, None]
    packed_xT = pack_weight(n((K, T)) * s)
    return {
        "x_words": packed_xT[0],
        "x_scales": packed_xT[1],
        "hT": (n((K, J)) / np.sqrt(K) / s).astype(np.float32),
        "gain": (np.tile(np.random.uniform(0.5, 1.5, T), (P, 1))).astype(np.float32),
        "shift": (np.tile(0.5 * np.random.standard_normal(T), (P, 1))).astype(np.float32),
        "offs": striped(np.random.permutation(T)[:S]),
    }


def reference(x_words, x_scales, hT, gain, shift, offs):
    hTq = mxq(f64(hT), 0, "e4m3")
    xq = unpack_weight(x_words, x_scales)[:, unstriped(offs)]
    y = hTq.T @ xq
    g = f64(gain)[:1][:, unstriped(offs)]
    s_ = f64(shift)[:1][:, unstriped(offs)]
    z = y * g + s_
    e = np.exp(z - z.max(axis=1, keepdims=True))
    return e / e.sum(axis=1, keepdims=True)

@@ -1,0 +1,130 @@
+from contextlib import ExitStack
+
+import concourse.mybir as mybir
+from concourse.masks import make_identity
+
+F32 = mybir.dt.float32
+BF16 = mybir.dt.bfloat16
+I32 = mybir.dt.int32
+U32 = mybir.dt.uint32
+U16 = mybir.dt.uint16
+U8 = mybir.dt.uint8
+FP8X4 = mybir.dt.float8_e4m3fn_x4
+ALU = mybir.AluOpType
+ACT = mybir.ActivationFunctionType
+AX = mybir.AxisListType
+
+P = 128
+PACK = 4
+K, T, S, J = 512, 1024, 512, 512
+HALF = J // 2
+CHUNKS = S // P
+FLOPS = 2 * K * S * J
+BYTES = K * T + 16 * T + 4 * K * J + 2 * 4 * T + 2 * S + 4 * J * S
+
+
+def tile_picked_zplatt_soft_p_kernel(tc, x_words, x_scales, hT, gain, shift, offs, out):
+    nc = tc.nc
+    with ExitStack() as ctx:
+        keep = ctx.enter_context(tc.tile_pool(name="keep", bufs=1))
+        stats = ctx.enter_context(tc.tile_pool(name="stats", bufs=3))
+        psum = ctx.enter_context(tc.psum_pool(name="psum", bufs=1))
+
+        offsets = keep.tile([P, S // 16], U16, name="offsets")
+        scale_win = keep.tile([P, T], U8, name="scale_win", align_bytes=64)
+        calib_win = keep.tile([P, T], F32, name="calib_win", align_bytes=64)
+        word_win = keep.tile([P, T], U32, name="word_win", align_bytes=64)
+        h_raw = [keep.tile([P, PACK, HALF], F32, name="h_raw%d" % h, align_bytes=64) for h in range(2)]
+
+        nc.vector.memset(calib_win[0 : P - 2, :], 0.0)
+
+        h_rows = hT.rearrange("(p j) t -> p j t", j=PACK)
+        nc.sync.dma_start(offsets[:], offs)
+        for q in range(4):
+            queue = nc.sync if q % 2 else nc.scalar
+            queue.dma_start(
+                scale_win[32 * q : 32 * q + 32, :].bitcast(I32),
+                x_scales[0, 4 * q : 4 * q + 4, :].bitcast(I32).partition_broadcast(8),
+            )
+        nc.scalar.dma_start(calib_win[P - 2 : P - 1, :], gain[0:1, :])
+        nc.sync.dma_start(calib_win[P - 1 : P, :], shift[0:1, :])
+        nc.sync.dma_start(h_raw[0][:], h_rows[:, :, 0:HALF])
+        nc.sync.dma_start(word_win[:].bitcast(I32), x_words[0].rearrange("p n t -> p (n t)").bitcast(I32))
+        nc.sync.dma_start(h_raw[1][:], h_rows[:, :, HALF:J])
+
+        warm = keep.tile([P, 2], F32, name="warm")
+        nc.gpsimd.memset(warm[:, 0:1], 0.0)
+        nc.scalar.activation(warm[:, 1:2], warm[:, 0:1], ACT.Exp)
+
+        ident = keep.tile([P, P], F32, name="ident")
+        make_identity(nc, ident[:])
+
+        x_scl = keep.tile([P, S], U8, name="x_scl", align_bytes=64)
+        calib = keep.tile([P, S], F32, name="calib", align_bytes=64)
+        x_codes = keep.tile([P, S], U32, name="x_codes", align_bytes=64)
+        nc.vector.tensor_copy(x_scl[:], scale_win[:].indirect(offsets[:]))
+        nc.vector.tensor_copy(calib[:], calib_win[:].indirect(offsets[:]))
+
+        calib_col = keep.tile([P, CHUNKS, 2], F32, name="calib_col")
+        for c in range(CHUNKS):
+            calib_ps = psum.tile([P, P], F32, name="calib_ps%d" % c, tag="y%d" % c)
+            nc.tensor.transpose(calib_ps[:], calib[:, c * P : (c + 1) * P], ident[:])
+            nc.scalar.copy(calib_col[:, c, :], calib_ps[:, P - 2 : P])
+
+        def quantize_half(h, interleave):
+            grouped = keep.tile([P, HALF, PACK], BF16, name="grouped%d" % h, align_bytes=64)
+            interleave(
+                grouped[:].rearrange("p (c i) t -> p c t i", i=4),
+                h_raw[h][:].rearrange("p t (c i) -> p c t i", i=4),
+            )
+            codes = keep.tile([P, HALF], U32, name="h_codes%d" % h, align_bytes=64)
+            scl = keep.tile([P, HALF], U8, name="h_scl%d" % h, align_bytes=64)
+            nc.vector.quantize_mx(out=codes[:].bitcast(FP8X4), scales=scl[:], in_=grouped[:].rearrange("p w t -> p (w t)"))
+            return codes, scl
+
+        def logits_half(h, codes, scl):
+            zt = keep.tile([P, CHUNKS, HALF], F32, name="z_t%d" % h, align_bytes=64)
+            for pair in range(2):
+                y = psum.tile([P, 2, HALF], F32, name="y%d%d" % (h, pair), tag="y%d" % (2 * h + pair))
+                for u in range(2):
+                    c = 2 * pair + u
+                    cols = slice(c * P, (c + 1) * P)
+                    nc.tensor.matmul_mx(
+                        out=y[:, u, :],
+                        lhsT=x_codes[:, cols].bitcast(FP8X4),
+                        lhsT_scale=x_scl[:, cols],
+                        rhs=codes[:].bitcast(FP8X4),
+                        rhs_scale=scl[:],
+                        start=True,
+                        stop=True,
+                    )
+                for u in range(2):
+                    c = 2 * pair + u
+                    nc.scalar.activation(zt[:, c, :], y[:, u, :], ACT.Identity, bias=calib_col[:, c, 1:2], scale=calib_col[:, c, 0:1])
+            return zt
+
+        def softmax_tile(d, zt):
+            u = d % 2
+            z = psum.tile([P, S], F32, name="z%d" % d)
+            for c in range(CHUNKS):
+                nc.tensor.transpose(z[:, c * P : (c + 1) * P], zt[:, c, u * P : (u + 1) * P], ident[:])
+            stat = stats.tile([P, 4], F32, name="stat")
+            neg_max, total, inv = stat[:, 0:1], stat[:, 1:2], stat[:, 2:3]
+            nc.vector.tensor_reduce(neg_max, z[:], AX.X, ALU.max, negate=True)
+            e = keep.tile([P, S], F32, name="e%d" % d)
+            nc.scalar.activation(e[:], z[:], ACT.Exp, bias=neg_max, scale=1.0, accum_out=total)
+            nc.vector.reciprocal(inv, total)
+            prob = keep.tile([P, S], F32, name="prob%d" % d)
+            nc.vector.tensor_scalar(prob[:], e[:], inv, None, ALU.mult)
+            nc.sync.dma_start(out[d * P : (d + 1) * P, :], prob[:])
+
+        first = quantize_half(0, nc.scalar.copy)
+        for c in range(CHUNKS):
+            nc.vector.tensor_copy(x_codes[:, c * P : (c + 1) * P], word_win[:].indirect(offsets[:, c * 8 : (c + 1) * 8]))
+        zt0 = logits_half(0, *first)
+        second = quantize_half(1, nc.vector.tensor_copy)
+        softmax_tile(0, zt0)
+        zt1 = logits_half(1, *second)
+        softmax_tile(1, zt0)
+        softmax_tile(2, zt1)
+        softmax_tile(3, zt1)

@@ -34,7 +34,7 @@ def tile_picked_zplatt_soft_p_kernel(tc, x_words, x_scales, hT, gain, shift, off
         scale_win = keep.tile([P, T], U8, name="scale_win", align_bytes=64)
         calib_win = keep.tile([P, T], F32, name="calib_win", align_bytes=64)
         word_win = keep.tile([P, T], U32, name="word_win", align_bytes=64)
-        h_raw = [keep.tile([P, PACK, HALF], F32, name="h_raw%d" % h, align_bytes=64) for h in range(2)]
+        h_raw = [keep.tile([P, PACK, HALF], F32, name="h_raw%d" % h, tag="h_raw%d" % h, align_bytes=64) for h in range(2)]
 
         nc.vector.memset(calib_win[0 : P - 2, :], 0.0)
 
@@ -48,8 +48,8 @@ def tile_picked_zplatt_soft_p_kernel(tc, x_words, x_scales, hT, gain, shift, off
             )
         nc.scalar.dma_start(calib_win[P - 2 : P - 1, :], gain[0:1, :])
         nc.sync.dma_start(calib_win[P - 1 : P, :], shift[0:1, :])
-        nc.sync.dma_start(h_raw[0][:], h_rows[:, :, 0:HALF])
         nc.sync.dma_start(word_win[:].bitcast(I32), x_words[0].rearrange("p n t -> p (n t)").bitcast(I32))
+        nc.sync.dma_start(h_raw[0][:], h_rows[:, :, 0:HALF])
         nc.sync.dma_start(h_raw[1][:], h_rows[:, :, HALF:J])
 
         warm = keep.tile([P, 2], F32, name="warm")
@@ -60,47 +60,65 @@ def tile_picked_zplatt_soft_p_kernel(tc, x_words, x_scales, hT, gain, shift, off
         make_identity(nc, ident[:])
 
         x_scl = keep.tile([P, S], U8, name="x_scl", align_bytes=64)
-        calib = keep.tile([P, S], F32, name="calib", align_bytes=64)
-        x_codes = keep.tile([P, S], U32, name="x_codes", align_bytes=64)
+        calib = keep.tile([P, S], F32, name="calib", tag="h_codes0", align_bytes=64)
         nc.vector.tensor_copy(x_scl[:], scale_win[:].indirect(offsets[:]))
         nc.vector.tensor_copy(calib[:], calib_win[:].indirect(offsets[:]))
 
-        calib_col = keep.tile([P, CHUNKS, 2], F32, name="calib_col")
+        calib_ps = psum.tile([P, CHUNKS, P], F32, name="calib_ps", tag="y2")
         for c in range(CHUNKS):
-            calib_ps = psum.tile([P, P], F32, name="calib_ps%d" % c, tag="y%d" % c)
-            nc.tensor.transpose(calib_ps[:], calib[:, c * P : (c + 1) * P], ident[:])
-            nc.scalar.copy(calib_col[:, c, :], calib_ps[:, P - 2 : P])
+            nc.tensor.transpose(calib_ps[:, c, :], calib[:, c * P : (c + 1) * P], ident[:])
 
-        def quantize_half(h, interleave):
-            grouped = keep.tile([P, HALF, PACK], BF16, name="grouped%d" % h, align_bytes=64)
-            interleave(
-                grouped[:].rearrange("p (c i) t -> p c t i", i=4),
-                h_raw[h][:].rearrange("p t (c i) -> p c t i", i=4),
+        x_codes = keep.tile([P, S], U32, name="x_codes", align_bytes=64)
+        nc.vector.tensor_copy(x_codes[:], word_win[:].indirect(offsets[:]))
+
+        def interleave(grouped, h, docs, copy):
+            copy(
+                grouped[:, docs, :].rearrange("p (c i) t -> p c t i", i=4),
+                h_raw[h][:, :, docs].rearrange("p t (c i) -> p c t i", i=4),
             )
-            codes = keep.tile([P, HALF], U32, name="h_codes%d" % h, align_bytes=64)
-            scl = keep.tile([P, HALF], U8, name="h_scl%d" % h, align_bytes=64)
-            nc.vector.quantize_mx(out=codes[:].bitcast(FP8X4), scales=scl[:], in_=grouped[:].rearrange("p w t -> p (w t)"))
-            return codes, scl
 
-        def logits_half(h, codes, scl):
+        def quantize(grouped, h, docs):
+            nc.vector.quantize_mx(
+                out=h_codes[h][:, docs].bitcast(FP8X4),
+                scales=h_scl[h][:, docs],
+                in_=grouped[:, docs, :].rearrange("p w t -> p (w t)"),
+            )
+
+        h_codes = [keep.tile([P, HALF], U32, name="h_codes%d" % h, tag="h_codes%d" % h, align_bytes=64) for h in range(2)]
+        h_scl = [keep.tile([P, HALF], U8, name="h_scl%d" % h, align_bytes=64) for h in range(2)]
+        h_bf = [keep.tile([P, HALF, PACK], BF16, name="h_bf%d" % h, align_bytes=64) for h in range(2)]
+        for docs in (slice(0, P), slice(P, HALF)):
+            interleave(h_bf[0], 0, docs, nc.scalar.copy)
+            quantize(h_bf[0], 0, docs)
+
+        calib_col = keep.tile([P, CHUNKS, 2], F32, name="calib_col", tag="h_raw0", align_bytes=64)
+        nc.scalar.copy(calib_col[:], calib_ps[:, :, P - 2 : P])
+
+        interleave(h_bf[1], 1, slice(0, P), nc.scalar.copy)
+        interleave(h_bf[1], 1, slice(P, HALF), nc.vector.tensor_copy)
+        quantize(h_bf[1], 1, slice(0, HALF))
+
+        def logits_half(h, pieces):
             zt = keep.tile([P, CHUNKS, HALF], F32, name="z_t%d" % h, align_bytes=64)
-            for pair in range(2):
-                y = psum.tile([P, 2, HALF], F32, name="y%d%d" % (h, pair), tag="y%d" % (2 * h + pair))
-                for u in range(2):
-                    c = 2 * pair + u
+            y = [psum.tile([P, 2, HALF], F32, name="y%d%d" % (h, pair), tag="y%d" % (2 * h + pair)) for pair in range(2)]
+            for docs in pieces:
+                for c in range(CHUNKS):
                     cols = slice(c * P, (c + 1) * P)
                     nc.tensor.matmul_mx(
-                        out=y[:, u, :],
+                        out=y[c // 2][:, c % 2, docs],
                         lhsT=x_codes[:, cols].bitcast(FP8X4),
                         lhsT_scale=x_scl[:, cols],
-                        rhs=codes[:].bitcast(FP8X4),
-                        rhs_scale=scl[:],
+                        rhs=h_codes[h][:, docs].bitcast(FP8X4),
+                        rhs_scale=h_scl[h][:, docs],
                         start=True,
                         stop=True,
                     )
-                for u in range(2):
-                    c = 2 * pair + u
-                    nc.scalar.activation(zt[:, c, :], y[:, u, :], ACT.Identity, bias=calib_col[:, c, 1:2], scale=calib_col[:, c, 0:1])
+            for c in range(CHUNKS):
+                slope, offset = calib_col[:, c, 0:1], calib_col[:, c, 1:2]
+                if h == 0 and c >= 2:
+                    nc.vector.tensor_scalar(zt[:, c, :], y[c // 2][:, c % 2, :], slope, offset, ALU.mult, ALU.add)
+                else:
+                    nc.scalar.activation(zt[:, c, :], y[c // 2][:, c % 2, :], ACT.Identity, bias=offset, scale=slope)
             return zt
 
         def softmax_tile(d, zt):
@@ -108,23 +126,24 @@ def tile_picked_zplatt_soft_p_kernel(tc, x_words, x_scales, hT, gain, shift, off
             z = psum.tile([P, S], F32, name="z%d" % d)
             for c in range(CHUNKS):
                 nc.tensor.transpose(z[:, c * P : (c + 1) * P], zt[:, c, u * P : (u + 1) * P], ident[:])
-            stat = stats.tile([P, 4], F32, name="stat")
-            neg_max, total, inv = stat[:, 0:1], stat[:, 1:2], stat[:, 2:3]
+            stat = stats.tile([P, 2], F32, name="stat")
+            neg_max, total = stat[:, 0:1], stat[:, 1:2]
+            inv_tile = keep.tile([P, 1], F32, name="inv%d" % d)
+            inv = inv_tile[:]
             nc.vector.tensor_reduce(neg_max, z[:], AX.X, ALU.max, negate=True)
             e = keep.tile([P, S], F32, name="e%d" % d)
             nc.scalar.activation(e[:], z[:], ACT.Exp, bias=neg_max, scale=1.0, accum_out=total)
             nc.vector.reciprocal(inv, total)
             prob = keep.tile([P, S], F32, name="prob%d" % d)
-            nc.vector.tensor_scalar(prob[:], e[:], inv, None, ALU.mult)
+            if d == 0:
+                nc.gpsimd.tensor_scalar(prob[:], e[:], inv, 0.0, ALU.mult, ALU.add)
+            else:
+                nc.vector.tensor_scalar(prob[:], e[:], inv, None, ALU.mult)
             nc.sync.dma_start(out[d * P : (d + 1) * P, :], prob[:])
 
-        first = quantize_half(0, nc.scalar.copy)
-        for c in range(CHUNKS):
-            nc.vector.tensor_copy(x_codes[:, c * P : (c + 1) * P], word_win[:].indirect(offsets[:, c * 8 : (c + 1) * 8]))
-        zt0 = logits_half(0, *first)
-        second = quantize_half(1, nc.vector.tensor_copy)
+        zt0 = logits_half(0, (slice(0, P), slice(P, HALF)))
+        zt1 = logits_half(1, (slice(0, HALF),))
         softmax_tile(0, zt0)
-        zt1 = logits_half(1, *second)
         softmax_tile(1, zt0)
         softmax_tile(2, zt1)
         softmax_tile(3, zt1)

@@ -52,10 +52,6 @@ def tile_picked_zplatt_soft_p_kernel(tc, x_words, x_scales, hT, gain, shift, off
         nc.sync.dma_start(h_raw[0][:], h_rows[:, :, 0:HALF])
         nc.sync.dma_start(h_raw[1][:], h_rows[:, :, HALF:J])
 
-        warm = keep.tile([P, 2], F32, name="warm")
-        nc.gpsimd.memset(warm[:, 0:1], 0.0)
-        nc.scalar.activation(warm[:, 1:2], warm[:, 0:1], ACT.Exp)
-
         ident = keep.tile([P, P], F32, name="ident")
         make_identity(nc, ident[:])
 
@@ -70,6 +66,9 @@ def tile_picked_zplatt_soft_p_kernel(tc, x_words, x_scales, hT, gain, shift, off
 
         x_codes = keep.tile([P, S], U32, name="x_codes", align_bytes=64)
         nc.vector.tensor_copy(x_codes[:], word_win[:].indirect(offsets[:]))
+
+        def scalar_cast(dst, src):
+            nc.scalar.activation(dst, src, ACT.Identity)
 
         def interleave(grouped, h, docs, copy):
             copy(
@@ -88,13 +87,13 @@ def tile_picked_zplatt_soft_p_kernel(tc, x_words, x_scales, hT, gain, shift, off
         h_scl = [keep.tile([P, HALF], U8, name="h_scl%d" % h, align_bytes=64) for h in range(2)]
         h_bf = [keep.tile([P, HALF, PACK], BF16, name="h_bf%d" % h, align_bytes=64) for h in range(2)]
         for docs in (slice(0, P), slice(P, HALF)):
-            interleave(h_bf[0], 0, docs, nc.scalar.copy)
+            interleave(h_bf[0], 0, docs, scalar_cast)
             quantize(h_bf[0], 0, docs)
 
         calib_col = keep.tile([P, CHUNKS, 2], F32, name="calib_col", tag="h_raw0", align_bytes=64)
         nc.scalar.copy(calib_col[:], calib_ps[:, :, P - 2 : P])
 
-        interleave(h_bf[1], 1, slice(0, P), nc.scalar.copy)
+        interleave(h_bf[1], 1, slice(0, P), scalar_cast)
         interleave(h_bf[1], 1, slice(P, HALF), nc.vector.tensor_copy)
         quantize(h_bf[1], 1, slice(0, HALF))
 

@@ -27,52 +27,52 @@ def tile_picked_zplatt_soft_p_kernel(tc, x_words, x_scales, hT, gain, shift, off
     nc = tc.nc
     with ExitStack() as ctx:
         keep = ctx.enter_context(tc.tile_pool(name="keep", bufs=1))
-        stats = ctx.enter_context(tc.tile_pool(name="stats", bufs=3))
+        arena = ctx.enter_context(tc.tile_pool(name="arena", bufs=1))
         psum = ctx.enter_context(tc.psum_pool(name="psum", bufs=1))
 
         offsets = keep.tile([P, S // 16], U16, name="offsets")
-        scale_win = keep.tile([P, T], U8, name="scale_win", align_bytes=64)
+        scale_win = arena.tile([P, T], U8, name="scale_win", align_bytes=64, offset=0)
         calib_win = keep.tile([P, T], F32, name="calib_win", align_bytes=64)
         word_win = keep.tile([P, T], U32, name="word_win", align_bytes=64)
-        h_raw = [keep.tile([P, PACK, HALF], F32, name="h_raw%d" % h, tag="h_raw%d" % h, align_bytes=64) for h in range(2)]
+        h_raw = [
+            arena.tile([P, PACK, HALF], F32, name="h_raw0", align_bytes=64, offset=3072),
+            keep.tile([P, PACK, HALF], F32, name="h_raw1", align_bytes=64),
+        ]
 
         nc.vector.memset(calib_win[0 : P - 2, :], 0.0)
 
         h_rows = hT.rearrange("(p j) t -> p j t", j=PACK)
         nc.sync.dma_start(offsets[:], offs)
+        nc.scalar.dma_start(calib_win[P - 2 : P - 1, :], gain[0:1, :])
+        nc.sync.dma_start(calib_win[P - 1 : P, :], shift[0:1, :])
         for q in range(4):
             queue = nc.sync if q % 2 else nc.scalar
             queue.dma_start(
                 scale_win[32 * q : 32 * q + 32, :].bitcast(I32),
                 x_scales[0, 4 * q : 4 * q + 4, :].bitcast(I32).partition_broadcast(8),
             )
-        nc.scalar.dma_start(calib_win[P - 2 : P - 1, :], gain[0:1, :])
-        nc.sync.dma_start(calib_win[P - 1 : P, :], shift[0:1, :])
-        nc.sync.dma_start(word_win[:].bitcast(I32), x_words[0].rearrange("p n t -> p (n t)").bitcast(I32))
         nc.sync.dma_start(h_raw[0][:], h_rows[:, :, 0:HALF])
+        nc.sync.dma_start(word_win[:].bitcast(I32), x_words[0].rearrange("p n t -> p (n t)").bitcast(I32))
         nc.sync.dma_start(h_raw[1][:], h_rows[:, :, HALF:J])
 
         ident = keep.tile([P, P], F32, name="ident")
         make_identity(nc, ident[:])
 
         x_scl = keep.tile([P, S], U8, name="x_scl", align_bytes=64)
-        calib = keep.tile([P, S], F32, name="calib", tag="h_codes0", align_bytes=64)
-        nc.vector.tensor_copy(x_scl[:], scale_win[:].indirect(offsets[:]))
+        calib = arena.tile([P, S], F32, name="calib", align_bytes=64, offset=1024)
         nc.vector.tensor_copy(calib[:], calib_win[:].indirect(offsets[:]))
+        nc.vector.tensor_copy(x_scl[:], scale_win[:].indirect(offsets[:]))
 
-        calib_ps = psum.tile([P, CHUNKS, P], F32, name="calib_ps", tag="y2")
+        calib_ps = psum.tile([P, CHUNKS, P], F32, name="calib_ps", tag="bank7")
         for c in range(CHUNKS):
             nc.tensor.transpose(calib_ps[:, c, :], calib[:, c * P : (c + 1) * P], ident[:])
-
-        x_codes = keep.tile([P, S], U32, name="x_codes", align_bytes=64)
-        nc.vector.tensor_copy(x_codes[:], word_win[:].indirect(offsets[:]))
 
         def scalar_cast(dst, src):
             nc.scalar.activation(dst, src, ACT.Identity)
 
         def interleave(grouped, h, docs, copy):
             copy(
-                grouped[:, docs, :].rearrange("p (c i) t -> p c t i", i=4),
+                grouped.rearrange("p (c i) t -> p c t i", i=4),
                 h_raw[h][:, :, docs].rearrange("p t (c i) -> p c t i", i=4),
             )
 
@@ -80,69 +80,114 @@ def tile_picked_zplatt_soft_p_kernel(tc, x_words, x_scales, hT, gain, shift, off
             nc.vector.quantize_mx(
                 out=h_codes[h][:, docs].bitcast(FP8X4),
                 scales=h_scl[h][:, docs],
-                in_=grouped[:, docs, :].rearrange("p w t -> p (w t)"),
+                in_=grouped.rearrange("p w t -> p (w t)"),
             )
 
-        h_codes = [keep.tile([P, HALF], U32, name="h_codes%d" % h, tag="h_codes%d" % h, align_bytes=64) for h in range(2)]
+        first, second, both = slice(0, P), slice(P, HALF), slice(0, HALF)
+        h_codes = [
+            arena.tile([P, HALF], U32, name="h_codes0", align_bytes=64, offset=1536),
+            keep.tile([P, HALF], U32, name="h_codes1", align_bytes=64),
+        ]
         h_scl = [keep.tile([P, HALF], U8, name="h_scl%d" % h, align_bytes=64) for h in range(2)]
-        h_bf = [keep.tile([P, HALF, PACK], BF16, name="h_bf%d" % h, align_bytes=64) for h in range(2)]
-        for docs in (slice(0, P), slice(P, HALF)):
-            interleave(h_bf[0], 0, docs, scalar_cast)
-            quantize(h_bf[0], 0, docs)
 
-        calib_col = keep.tile([P, CHUNKS, 2], F32, name="calib_col", tag="h_raw0", align_bytes=64)
+        x_early = arena.tile([P, HALF], U32, name="x_early", align_bytes=64, offset=512)
+        nc.vector.tensor_copy(x_early[:], word_win[:].indirect(offsets[:, 0:16]))
+
+        h_bf0 = keep.tile([P, P, PACK], BF16, name="h_bf0", align_bytes=64)
+        interleave(h_bf0[:], 0, first, scalar_cast)
+        quantize(h_bf0[:], 0, first)
+        h_bf1 = keep.tile([P, P, PACK], BF16, name="h_bf1", tag="h_bf1", align_bytes=64)
+        interleave(h_bf1[:], 0, second, scalar_cast)
+        quantize(h_bf1[:], 0, second)
+
+        calib_col = arena.tile([P, CHUNKS, 2], F32, name="calib_col", align_bytes=64, offset=3584)
         nc.scalar.copy(calib_col[:], calib_ps[:, :, P - 2 : P])
 
-        interleave(h_bf[1], 1, slice(0, P), scalar_cast)
-        interleave(h_bf[1], 1, slice(P, HALF), nc.vector.tensor_copy)
-        quantize(h_bf[1], 1, slice(0, HALF))
+        x_late = arena.tile([P, HALF], U32, name="x_late", align_bytes=64, offset=2560)
+        nc.vector.tensor_copy(x_late[:], word_win[:].indirect(offsets[:, 16:32]))
+        x_codes = [x_early, x_late]
 
-        def logits_half(h, pieces):
-            zt = keep.tile([P, CHUNKS, HALF], F32, name="z_t%d" % h, align_bytes=64)
-            y = [psum.tile([P, 2, HALF], F32, name="y%d%d" % (h, pair), tag="y%d" % (2 * h + pair)) for pair in range(2)]
-            for docs in pieces:
-                for c in range(CHUNKS):
-                    cols = slice(c * P, (c + 1) * P)
-                    nc.tensor.matmul_mx(
-                        out=y[c // 2][:, c % 2, docs],
-                        lhsT=x_codes[:, cols].bitcast(FP8X4),
-                        lhsT_scale=x_scl[:, cols],
-                        rhs=h_codes[h][:, docs].bitcast(FP8X4),
-                        rhs_scale=h_scl[h][:, docs],
-                        start=True,
-                        stop=True,
-                    )
-            for c in range(CHUNKS):
-                slope, offset = calib_col[:, c, 0:1], calib_col[:, c, 1:2]
-                if h == 0 and c >= 2:
-                    nc.vector.tensor_scalar(zt[:, c, :], y[c // 2][:, c % 2, :], slope, offset, ALU.mult, ALU.add)
-                else:
-                    nc.scalar.activation(zt[:, c, :], y[c // 2][:, c % 2, :], ACT.Identity, bias=offset, scale=slope)
-            return zt
+        h_bf2 = keep.tile([P, P, PACK], BF16, name="h_bf2", align_bytes=64)
+        interleave(h_bf2[:], 1, first, scalar_cast)
+        h_bf3 = keep.tile([P, P, PACK], BF16, name="h_bf3", tag="h_bf1", align_bytes=64)
+        interleave(h_bf3[:], 1, second, nc.vector.tensor_copy)
+        quantize(h_bf2[:], 1, first)
+        quantize(h_bf3[:], 1, second)
 
-        def softmax_tile(d, zt):
-            u = d % 2
-            z = psum.tile([P, S], F32, name="z%d" % d)
-            for c in range(CHUNKS):
-                nc.tensor.transpose(z[:, c * P : (c + 1) * P], zt[:, c, u * P : (u + 1) * P], ident[:])
-            stat = stats.tile([P, 2], F32, name="stat")
-            neg_max, total = stat[:, 0:1], stat[:, 1:2]
-            inv_tile = keep.tile([P, 1], F32, name="inv%d" % d)
-            inv = inv_tile[:]
-            nc.vector.tensor_reduce(neg_max, z[:], AX.X, ALU.max, negate=True)
-            e = keep.tile([P, S], F32, name="e%d" % d)
-            nc.scalar.activation(e[:], z[:], ACT.Exp, bias=neg_max, scale=1.0, accum_out=total)
-            nc.vector.reciprocal(inv, total)
-            prob = keep.tile([P, S], F32, name="prob%d" % d)
-            if d == 0:
-                nc.gpsimd.tensor_scalar(prob[:], e[:], inv, 0.0, ALU.mult, ALU.add)
+        warm = psum.tile([P, 2, HALF], F32, name="warm", tag="bank6")
+        for i in range(2):
+            nc.tensor.matmul_mx(
+                out=warm[:, i, :],
+                lhsT=x_early[:, 0:P].bitcast(FP8X4),
+                lhsT_scale=x_scl[:, 0:P],
+                rhs=x_early[:].bitcast(FP8X4),
+                rhs_scale=x_scl[:, 0:HALF],
+                start=True,
+                stop=True,
+            )
+
+        zt = [keep.tile([P, CHUNKS, HALF], F32, name="z_t%d" % h, align_bytes=64) for h in range(2)]
+
+        def product_banks(name, width, banks):
+            tiles = {b: psum.tile([P, banks.count(b), width], F32, name="%s_%d" % (name, b), tag="bank%d" % b) for b in set(banks)}
+            return [tiles[b][:, banks[:c].count(b), :] for c, b in enumerate(banks)]
+
+        def product(y, h, docs, c):
+            nc.tensor.matmul_mx(
+                out=y[c],
+                lhsT=x_codes[c // 2][:, (c % 2) * P : (c % 2 + 1) * P].bitcast(FP8X4),
+                lhsT_scale=x_scl[:, c * P : (c + 1) * P],
+                rhs=h_codes[h][:, docs].bitcast(FP8X4),
+                rhs_scale=h_scl[h][:, docs],
+                start=True,
+                stop=True,
+            )
+
+        def affine(y, h, docs, c, on_vector):
+            slope, offset = calib_col[:, c, 0:1], calib_col[:, c, 1:2]
+            if on_vector:
+                nc.vector.tensor_scalar(zt[h][:, c, docs], y[c], slope, offset, ALU.mult, ALU.add)
             else:
-                nc.vector.tensor_scalar(prob[:], e[:], inv, None, ALU.mult)
+                nc.scalar.activation(zt[h][:, c, docs], y[c], ACT.Identity, bias=offset, scale=slope)
+
+        def turn_and_max(d, bank):
+            h, u = divmod(d, 2)
+            z = psum.tile([P, S], F32, name="z%d" % d, tag="bank%d" % bank)
+            for c in range(CHUNKS):
+                nc.tensor.transpose(z[:, c * P : (c + 1) * P], zt[h][:, c, u * P : (u + 1) * P], ident[:])
+            neg_max = keep.tile([P, 1], F32, name="neg_max%d" % d)
+            nc.vector.tensor_reduce(neg_max[:], z[:], AX.X, ALU.max, negate=True)
+            return z, neg_max
+
+        def finish(d, z, neg_max):
+            total = keep.tile([P, 1], F32, name="total%d" % d)
+            inv = keep.tile([P, 1], F32, name="inv%d" % d)
+            e = keep.tile([P, S], F32, name="e%d" % d)
+            nc.scalar.activation(e[:], z[:], ACT.Exp, bias=neg_max[:], scale=1.0, accum_out=total[:])
+            nc.vector.reciprocal(inv[:], total[:])
+            prob = keep.tile([P, S], F32, name="prob%d" % d)
+            if d < 1:
+                nc.gpsimd.tensor_scalar(prob[:], e[:], inv[:], 0.0, ALU.mult, ALU.add)
+            else:
+                nc.vector.tensor_scalar(prob[:], e[:], inv[:], None, ALU.mult)
             nc.sync.dma_start(out[d * P : (d + 1) * P, :], prob[:])
 
-        zt0 = logits_half(0, (slice(0, P), slice(P, HALF)))
-        zt1 = logits_half(1, (slice(0, HALF),))
-        softmax_tile(0, zt0)
-        softmax_tile(1, zt0)
-        softmax_tile(2, zt1)
-        softmax_tile(3, zt1)
+        y_first = product_banks("y_first", P, [0, 0, 1, 1])
+        y_second = product_banks("y_second", P, [2, 2, 3, 4])
+        for pair in ((0, 1), (2, 3)):
+            for y, docs in ((y_first, first), (y_second, second)):
+                for c in pair:
+                    product(y, 0, docs, c)
+        for c in range(CHUNKS):
+            affine(y_first, 0, first, c, False)
+        for c in range(CHUNKS):
+            affine(y_second, 0, second, c, True)
+        tile0 = turn_and_max(0, 5)
+        y_late = product_banks("y_late", HALF, [1, 1, 4, 4])
+        for c in range(CHUNKS):
+            product(y_late, 1, both, c)
+        for c in range(CHUNKS):
+            affine(y_late, 1, both, c, c >= 2)
+        finish(0, *tile0)
+        for d, bank in ((1, 3), (2, 0), (3, 2)):
+            finish(d, *turn_and_max(d, bank))

@@ -35,8 +35,10 @@ def tile_picked_zplatt_soft_p_kernel(tc, x_words, x_scales, hT, gain, shift, off
         calib_win = keep.tile([P, T], F32, name="calib_win", align_bytes=64)
         word_win = keep.tile([P, T], U32, name="word_win", align_bytes=64)
         h_raw = [
-            arena.tile([P, PACK, HALF], F32, name="h_raw0", align_bytes=64, offset=3072),
-            keep.tile([P, PACK, HALF], F32, name="h_raw1", align_bytes=64),
+            arena.tile([P, PACK, P], F32, name="h_raw0", align_bytes=64, offset=3072),
+            arena.tile([P, PACK, P], F32, name="h_raw1", align_bytes=64, offset=6144),
+            keep.tile([P, PACK, P], F32, name="h_raw2", align_bytes=64),
+            keep.tile([P, PACK, P], F32, name="h_raw3", align_bytes=64),
         ]
 
         nc.vector.memset(calib_win[0 : P - 2, :], 0.0)
@@ -51,9 +53,9 @@ def tile_picked_zplatt_soft_p_kernel(tc, x_words, x_scales, hT, gain, shift, off
                 scale_win[32 * q : 32 * q + 32, :].bitcast(I32),
                 x_scales[0, 4 * q : 4 * q + 4, :].bitcast(I32).partition_broadcast(8),
             )
-        nc.sync.dma_start(h_raw[0][:], h_rows[:, :, 0:HALF])
         nc.sync.dma_start(word_win[:].bitcast(I32), x_words[0].rearrange("p n t -> p (n t)").bitcast(I32))
-        nc.sync.dma_start(h_raw[1][:], h_rows[:, :, HALF:J])
+        for d in range(4):
+            nc.sync.dma_start(h_raw[d][:], h_rows[:, :, d * P : (d + 1) * P])
 
         ident = keep.tile([P, P], F32, name="ident")
         make_identity(nc, ident[:])
@@ -70,10 +72,10 @@ def tile_picked_zplatt_soft_p_kernel(tc, x_words, x_scales, hT, gain, shift, off
         def scalar_cast(dst, src):
             nc.scalar.activation(dst, src, ACT.Identity)
 
-        def interleave(grouped, h, docs, copy):
+        def interleave(grouped, d, copy):
             copy(
                 grouped.rearrange("p (c i) t -> p c t i", i=4),
-                h_raw[h][:, :, docs].rearrange("p t (c i) -> p c t i", i=4),
+                h_raw[d][:].rearrange("p t (c i) -> p c t i", i=4),
             )
 
         def quantize(grouped, h, docs):
@@ -93,12 +95,9 @@ def tile_picked_zplatt_soft_p_kernel(tc, x_words, x_scales, hT, gain, shift, off
         x_early = arena.tile([P, HALF], U32, name="x_early", align_bytes=64, offset=512)
         nc.vector.tensor_copy(x_early[:], word_win[:].indirect(offsets[:, 0:16]))
 
-        h_bf0 = keep.tile([P, P, PACK], BF16, name="h_bf0", align_bytes=64)
-        interleave(h_bf0[:], 0, first, scalar_cast)
+        h_bf0 = arena.tile([P, P, PACK], BF16, name="h_bf0", align_bytes=64, offset=5120)
+        interleave(h_bf0[:], 0, scalar_cast)
         quantize(h_bf0[:], 0, first)
-        h_bf1 = keep.tile([P, P, PACK], BF16, name="h_bf1", tag="h_bf1", align_bytes=64)
-        interleave(h_bf1[:], 0, second, scalar_cast)
-        quantize(h_bf1[:], 0, second)
 
         calib_col = arena.tile([P, CHUNKS, 2], F32, name="calib_col", align_bytes=64, offset=3584)
         nc.scalar.copy(calib_col[:], calib_ps[:, :, P - 2 : P])
@@ -107,24 +106,31 @@ def tile_picked_zplatt_soft_p_kernel(tc, x_words, x_scales, hT, gain, shift, off
         nc.vector.tensor_copy(x_late[:], word_win[:].indirect(offsets[:, 16:32]))
         x_codes = [x_early, x_late]
 
+        h_bf1 = keep.tile([P, P, PACK], BF16, name="h_bf1", align_bytes=64)
+        interleave(h_bf1[:], 1, scalar_cast)
+        quantize(h_bf1[:], 0, second)
+
         h_bf2 = keep.tile([P, P, PACK], BF16, name="h_bf2", align_bytes=64)
-        interleave(h_bf2[:], 1, first, scalar_cast)
-        h_bf3 = keep.tile([P, P, PACK], BF16, name="h_bf3", tag="h_bf1", align_bytes=64)
-        interleave(h_bf3[:], 1, second, nc.vector.tensor_copy)
+        interleave(h_bf2[:], 2, scalar_cast)
+        h_bf3 = arena.tile([P, P, PACK], BF16, name="h_bf3", align_bytes=64, offset=5632)
+        interleave(h_bf3[:], 3, nc.vector.tensor_copy)
         quantize(h_bf2[:], 1, first)
         quantize(h_bf3[:], 1, second)
 
         warm = psum.tile([P, 2, HALF], F32, name="warm", tag="bank6")
-        for i in range(2):
+
+        def spare_pass(i, codes, scales):
             nc.tensor.matmul_mx(
                 out=warm[:, i, :],
-                lhsT=x_early[:, 0:P].bitcast(FP8X4),
-                lhsT_scale=x_scl[:, 0:P],
+                lhsT=codes.bitcast(FP8X4),
+                lhsT_scale=scales,
                 rhs=x_early[:].bitcast(FP8X4),
                 rhs_scale=x_scl[:, 0:HALF],
                 start=True,
                 stop=True,
             )
+
+        spare_pass(0, x_early[:, 0:P], x_scl[:, 0:P])
 
         zt = [keep.tile([P, CHUNKS, HALF], F32, name="z_t%d" % h, align_bytes=64) for h in range(2)]
 
@@ -174,20 +180,22 @@ def tile_picked_zplatt_soft_p_kernel(tc, x_words, x_scales, hT, gain, shift, off
 
         y_first = product_banks("y_first", P, [0, 0, 1, 1])
         y_second = product_banks("y_second", P, [2, 2, 3, 4])
-        for pair in ((0, 1), (2, 3)):
-            for y, docs in ((y_first, first), (y_second, second)):
-                for c in pair:
-                    product(y, 0, docs, c)
+        for c in range(CHUNKS):
+            if c == 2:
+                spare_pass(1, h_codes[0][:, first], h_scl[0][:, first])
+            product(y_first, 0, first, c)
+        for c in range(CHUNKS):
+            product(y_second, 0, second, c)
         for c in range(CHUNKS):
             affine(y_first, 0, first, c, False)
         for c in range(CHUNKS):
-            affine(y_second, 0, second, c, True)
+            affine(y_second, 0, second, c, c < 2)
         tile0 = turn_and_max(0, 5)
-        y_late = product_banks("y_late", HALF, [1, 1, 4, 4])
+        y_late = product_banks("y_late", HALF, [1, 1, 3, 3])
         for c in range(CHUNKS):
             product(y_late, 1, both, c)
         for c in range(CHUNKS):
             affine(y_late, 1, both, c, c >= 2)
         finish(0, *tile0)
-        for d, bank in ((1, 3), (2, 0), (3, 2)):
+        for d, bank in ((1, 4), (2, 0), (3, 2)):
             finish(d, *turn_and_max(d, bank))

@@ -31,7 +31,7 @@ def tile_picked_zplatt_soft_p_kernel(tc, x_words, x_scales, hT, gain, shift, off
         psum = ctx.enter_context(tc.psum_pool(name="psum", bufs=1))
 
         offsets = keep.tile([P, S // 16], U16, name="offsets")
-        scale_win = arena.tile([P, T], U8, name="scale_win", align_bytes=64, offset=0)
+        scale_win = keep.tile([P, T], U8, name="scale_win", align_bytes=64)
         calib_win = keep.tile([P, T], F32, name="calib_win", align_bytes=64)
         word_win = keep.tile([P, T], U32, name="word_win", align_bytes=64)
         h_raw = [
@@ -87,13 +87,17 @@ def tile_picked_zplatt_soft_p_kernel(tc, x_words, x_scales, hT, gain, shift, off
 
         first, second, both = slice(0, P), slice(P, HALF), slice(0, HALF)
         h_codes = [
-            arena.tile([P, HALF], U32, name="h_codes0", align_bytes=64, offset=1536),
+            keep.tile([P, HALF], U32, name="h_codes0", align_bytes=64),
             keep.tile([P, HALF], U32, name="h_codes1", align_bytes=64),
         ]
-        h_scl = [keep.tile([P, HALF], U8, name="h_scl%d" % h, align_bytes=64) for h in range(2)]
+        h_scl = [arena.tile([P, HALF], U8, name="h_scl%d" % h, align_bytes=64, offset=1088 + 256 * h) for h in range(2)]
 
-        x_early = arena.tile([P, HALF], U32, name="x_early", align_bytes=64, offset=512)
+        x_early = keep.tile([P, HALF], U32, name="x_early", align_bytes=64)
         nc.vector.tensor_copy(x_early[:], word_win[:].indirect(offsets[:, 0:16]))
+
+        x_late = keep.tile([P, HALF], U32, name="x_late", align_bytes=64)
+        nc.vector.tensor_copy(x_late[:], word_win[:].indirect(offsets[:, 16:32]))
+        x_codes = [x_early, x_late]
 
         h_bf0 = arena.tile([P, P, PACK], BF16, name="h_bf0", align_bytes=64, offset=5120)
         interleave(h_bf0[:], 0, scalar_cast)
@@ -102,22 +106,18 @@ def tile_picked_zplatt_soft_p_kernel(tc, x_words, x_scales, hT, gain, shift, off
         calib_col = arena.tile([P, CHUNKS, 2], F32, name="calib_col", align_bytes=64, offset=3584)
         nc.scalar.copy(calib_col[:], calib_ps[:, :, P - 2 : P])
 
-        x_late = arena.tile([P, HALF], U32, name="x_late", align_bytes=64, offset=2560)
-        nc.vector.tensor_copy(x_late[:], word_win[:].indirect(offsets[:, 16:32]))
-        x_codes = [x_early, x_late]
-
-        h_bf1 = keep.tile([P, P, PACK], BF16, name="h_bf1", align_bytes=64)
+        h_bf1 = arena.tile([P, P, PACK], BF16, name="h_bf1", align_bytes=64, offset=64)
         interleave(h_bf1[:], 1, scalar_cast)
         quantize(h_bf1[:], 0, second)
 
-        h_bf2 = keep.tile([P, P, PACK], BF16, name="h_bf2", align_bytes=64)
+        h_bf2 = arena.tile([P, P, PACK], BF16, name="h_bf2", align_bytes=64, offset=1600)
         interleave(h_bf2[:], 2, scalar_cast)
         h_bf3 = arena.tile([P, P, PACK], BF16, name="h_bf3", align_bytes=64, offset=5632)
         interleave(h_bf3[:], 3, nc.vector.tensor_copy)
         quantize(h_bf2[:], 1, first)
         quantize(h_bf3[:], 1, second)
 
-        warm = psum.tile([P, 2, HALF], F32, name="warm", tag="bank6")
+        warm = psum.tile([P, 2, HALF], F32, name="warm", tag="bank7")
 
         def spare_pass(i, codes, scales):
             nc.tensor.matmul_mx(
@@ -131,6 +131,7 @@ def tile_picked_zplatt_soft_p_kernel(tc, x_words, x_scales, hT, gain, shift, off
             )
 
         spare_pass(0, x_early[:, 0:P], x_scl[:, 0:P])
+        spare_pass(1, x_early[:, 0:P], x_scl[:, 0:P])
 
         zt = [keep.tile([P, CHUNKS, HALF], F32, name="z_t%d" % h, align_bytes=64) for h in range(2)]
 
@@ -181,8 +182,6 @@ def tile_picked_zplatt_soft_p_kernel(tc, x_words, x_scales, hT, gain, shift, off
         y_first = product_banks("y_first", P, [0, 0, 1, 1])
         y_second = product_banks("y_second", P, [2, 2, 3, 4])
         for c in range(CHUNKS):
-            if c == 2:
-                spare_pass(1, h_codes[0][:, first], h_scl[0][:, first])
             product(y_first, 0, first, c)
         for c in range(CHUNKS):
             product(y_second, 0, second, c)
@@ -191,11 +190,16 @@ def tile_picked_zplatt_soft_p_kernel(tc, x_words, x_scales, hT, gain, shift, off
         for c in range(CHUNKS):
             affine(y_second, 0, second, c, c < 2)
         tile0 = turn_and_max(0, 5)
-        y_late = product_banks("y_late", HALF, [1, 1, 3, 3])
+        y_third = product_banks("y_third", P, [1, 1, 0, 0])
+        y_fourth = product_banks("y_fourth", P, [3, 3, 4, 4])
         for c in range(CHUNKS):
-            product(y_late, 1, both, c)
+            product(y_third, 1, first, c)
         for c in range(CHUNKS):
-            affine(y_late, 1, both, c, c >= 2)
+            product(y_fourth, 1, second, c)
+        for c in range(CHUNKS):
+            affine(y_third, 1, first, c, c >= 2)
+        for c in range(CHUNKS):
+            affine(y_fourth, 1, second, c, c >= 2)
         finish(0, *tile0)
-        for d, bank in ((1, 4), (2, 0), (3, 2)):
+        for d, bank in ((1, 7), (2, 6), (3, 2)):
             finish(d, *turn_and_max(d, bank))

@@ -41,29 +41,31 @@ def tile_picked_zplatt_soft_p_kernel(tc, x_words, x_scales, hT, gain, shift, off
             keep.tile([P, PACK, P], F32, name="h_raw3", align_bytes=64),
         ]
 
+        nc.vector.memset(scale_win[:].bitcast(I32), 0)
         nc.vector.memset(calib_win[0 : P - 2, :], 0.0)
 
         h_rows = hT.rearrange("(p j) t -> p j t", j=PACK)
         nc.sync.dma_start(offsets[:], offs)
         nc.scalar.dma_start(calib_win[P - 2 : P - 1, :], gain[0:1, :])
         nc.sync.dma_start(calib_win[P - 1 : P, :], shift[0:1, :])
-        for q in range(4):
-            queue = nc.sync if q % 2 else nc.scalar
-            queue.dma_start(
-                scale_win[32 * q : 32 * q + 32, :].bitcast(I32),
-                x_scales[0, 4 * q : 4 * q + 4, :].bitcast(I32).partition_broadcast(8),
-            )
+
+        def load_scales(queue, q):
+            queue.dma_start(scale_win[32 * q : 32 * q + 4, :].bitcast(I32), x_scales[0, 4 * q : 4 * q + 4, :].bitcast(I32))
+
+        load_scales(nc.scalar, 0)
+        load_scales(nc.scalar, 1)
         nc.sync.dma_start(word_win[:].bitcast(I32), x_words[0].rearrange("p n t -> p (n t)").bitcast(I32))
-        for d in range(4):
+        nc.sync.dma_start(h_raw[0][:], h_rows[:, :, 0:P])
+        load_scales(nc.sync, 2)
+        load_scales(nc.sync, 3)
+        for d in range(1, 4):
             nc.sync.dma_start(h_raw[d][:], h_rows[:, :, d * P : (d + 1) * P])
 
         ident = keep.tile([P, P], F32, name="ident")
         make_identity(nc, ident[:])
 
-        x_scl = keep.tile([P, S], U8, name="x_scl", align_bytes=64)
         calib = arena.tile([P, S], F32, name="calib", align_bytes=64, offset=1024)
         nc.vector.tensor_copy(calib[:], calib_win[:].indirect(offsets[:]))
-        nc.vector.tensor_copy(x_scl[:], scale_win[:].indirect(offsets[:]))
 
         calib_ps = psum.tile([P, CHUNKS, P], F32, name="calib_ps", tag="bank7")
         for c in range(CHUNKS):
@@ -98,6 +100,9 @@ def tile_picked_zplatt_soft_p_kernel(tc, x_words, x_scales, hT, gain, shift, off
         x_late = keep.tile([P, HALF], U32, name="x_late", align_bytes=64)
         nc.vector.tensor_copy(x_late[:], word_win[:].indirect(offsets[:, 16:32]))
         x_codes = [x_early, x_late]
+        x_scl = [keep.tile([P, HALF], U8, name="x_scl%d" % h, align_bytes=64) for h in range(2)]
+        for h in range(2):
+            nc.vector.tensor_copy(x_scl[h][:], scale_win[:].indirect(offsets[:, 16 * h : 16 * h + 16]))
 
         h_bf0 = arena.tile([P, P, PACK], BF16, name="h_bf0", align_bytes=64, offset=5120)
         interleave(h_bf0[:], 0, scalar_cast)
@@ -106,7 +111,7 @@ def tile_picked_zplatt_soft_p_kernel(tc, x_words, x_scales, hT, gain, shift, off
         calib_col = arena.tile([P, CHUNKS, 2], F32, name="calib_col", align_bytes=64, offset=3584)
         nc.scalar.copy(calib_col[:], calib_ps[:, :, P - 2 : P])
 
-        h_bf1 = arena.tile([P, P, PACK], BF16, name="h_bf1", align_bytes=64, offset=64)
+        h_bf1 = keep.tile([P, P, PACK], BF16, name="h_bf1", align_bytes=64)
         interleave(h_bf1[:], 1, scalar_cast)
         quantize(h_bf1[:], 0, second)
 
@@ -125,13 +130,13 @@ def tile_picked_zplatt_soft_p_kernel(tc, x_words, x_scales, hT, gain, shift, off
                 lhsT=codes.bitcast(FP8X4),
                 lhsT_scale=scales,
                 rhs=x_early[:].bitcast(FP8X4),
-                rhs_scale=x_scl[:, 0:HALF],
+                rhs_scale=x_scl[0][:],
                 start=True,
                 stop=True,
             )
 
-        spare_pass(0, x_early[:, 0:P], x_scl[:, 0:P])
-        spare_pass(1, x_early[:, 0:P], x_scl[:, 0:P])
+        spare_pass(0, x_early[:, 0:P], x_scl[0][:, 0:P])
+        spare_pass(1, x_early[:, 0:P], x_scl[0][:, 0:P])
 
         zt = [keep.tile([P, CHUNKS, HALF], F32, name="z_t%d" % h, align_bytes=64) for h in range(2)]
 
@@ -143,7 +148,7 @@ def tile_picked_zplatt_soft_p_kernel(tc, x_words, x_scales, hT, gain, shift, off
             nc.tensor.matmul_mx(
                 out=y[c],
                 lhsT=x_codes[c // 2][:, (c % 2) * P : (c % 2 + 1) * P].bitcast(FP8X4),
-                lhsT_scale=x_scl[:, c * P : (c + 1) * P],
+                lhsT_scale=x_scl[c // 2][:, (c % 2) * P : (c % 2 + 1) * P],
                 rhs=h_codes[h][:, docs].bitcast(FP8X4),
                 rhs_scale=h_scl[h][:, docs],
                 start=True,

@@ -94,12 +94,9 @@ def tile_picked_zplatt_soft_p_kernel(tc, x_words, x_scales, hT, gain, shift, off
         ]
         h_scl = [arena.tile([P, HALF], U8, name="h_scl%d" % h, align_bytes=64, offset=1088 + 256 * h) for h in range(2)]
 
-        x_early = keep.tile([P, HALF], U32, name="x_early", align_bytes=64)
-        nc.vector.tensor_copy(x_early[:], word_win[:].indirect(offsets[:, 0:16]))
+        x_early = keep.tile([P, 3 * P], U32, name="x_early", align_bytes=64)
+        nc.vector.tensor_copy(x_early[:], word_win[:].indirect(offsets[:, 0:24]))
 
-        x_late = keep.tile([P, HALF], U32, name="x_late", align_bytes=64)
-        nc.vector.tensor_copy(x_late[:], word_win[:].indirect(offsets[:, 16:32]))
-        x_codes = [x_early, x_late]
         x_scl = [keep.tile([P, HALF], U8, name="x_scl%d" % h, align_bytes=64) for h in range(2)]
         for h in range(2):
             nc.vector.tensor_copy(x_scl[h][:], scale_win[:].indirect(offsets[:, 16 * h : 16 * h + 16]))
@@ -107,11 +104,14 @@ def tile_picked_zplatt_soft_p_kernel(tc, x_words, x_scales, hT, gain, shift, off
         h_bf0 = arena.tile([P, P, PACK], BF16, name="h_bf0", align_bytes=64, offset=5120)
         interleave(h_bf0[:], 0, scalar_cast)
         quantize(h_bf0[:], 0, first)
+        x_late = arena.tile([P, P], U32, name="x_late", align_bytes=64, offset=2624)
+        nc.vector.tensor_copy(x_late[:], word_win[:].indirect(offsets[:, 24:32]))
+        x_codes = [x_early[:, c * P : (c + 1) * P] for c in range(3)] + [x_late[:]]
 
         calib_col = arena.tile([P, CHUNKS, 2], F32, name="calib_col", align_bytes=64, offset=3584)
         nc.scalar.copy(calib_col[:], calib_ps[:, :, P - 2 : P])
 
-        h_bf1 = keep.tile([P, P, PACK], BF16, name="h_bf1", align_bytes=64)
+        h_bf1 = arena.tile([P, P, PACK], BF16, name="h_bf1", align_bytes=64, offset=64)
         interleave(h_bf1[:], 1, scalar_cast)
         quantize(h_bf1[:], 0, second)
 
@@ -129,7 +129,7 @@ def tile_picked_zplatt_soft_p_kernel(tc, x_words, x_scales, hT, gain, shift, off
                 out=warm[:, i, :],
                 lhsT=codes.bitcast(FP8X4),
                 lhsT_scale=scales,
-                rhs=x_early[:].bitcast(FP8X4),
+                rhs=x_early[:, 0:HALF].bitcast(FP8X4),
                 rhs_scale=x_scl[0][:],
                 start=True,
                 stop=True,
@@ -147,7 +147,7 @@ def tile_picked_zplatt_soft_p_kernel(tc, x_words, x_scales, hT, gain, shift, off
         def product(y, h, docs, c):
             nc.tensor.matmul_mx(
                 out=y[c],
-                lhsT=x_codes[c // 2][:, (c % 2) * P : (c % 2 + 1) * P].bitcast(FP8X4),
+                lhsT=x_codes[c].bitcast(FP8X4),
                 lhsT_scale=x_scl[c // 2][:, (c % 2) * P : (c % 2 + 1) * P],
                 rhs=h_codes[h][:, docs].bitcast(FP8X4),
                 rhs_scale=h_scl[h][:, docs],
@@ -184,7 +184,7 @@ def tile_picked_zplatt_soft_p_kernel(tc, x_words, x_scales, hT, gain, shift, off
                 nc.vector.tensor_scalar(prob[:], e[:], inv[:], None, ALU.mult)
             nc.sync.dma_start(out[d * P : (d + 1) * P, :], prob[:])
 
-        y_first = product_banks("y_first", P, [0, 0, 1, 1])
+        y_first = product_banks("y_first", P, [0, 0, 6, 1])
         y_second = product_banks("y_second", P, [2, 2, 3, 4])
         for c in range(CHUNKS):
             product(y_first, 0, first, c)

@@ -17,8 +17,8 @@ AX = mybir.AxisListType
 P = 128
 PACK = 4
 K, T, S, J = 512, 1024, 512, 512
-HALF = J // 2
 CHUNKS = S // P
+TILES = J // P
 FLOPS = 2 * K * S * J
 BYTES = K * T + 16 * T + 4 * K * J + 2 * 4 * T + 2 * S + 4 * J * S
 
@@ -32,41 +32,44 @@ def tile_picked_zplatt_soft_p_kernel(tc, x_words, x_scales, hT, gain, shift, off
 
         offsets = keep.tile([P, S // 16], U16, name="offsets")
         scale_win = keep.tile([P, T], U8, name="scale_win", align_bytes=64)
-        calib_win = keep.tile([P, T], F32, name="calib_win", align_bytes=64)
+        scale_odd = keep.tile([4, 2, T], U8, name="scale_odd", align_bytes=64)
+        calib_win = arena.tile([P, T], F32, name="calib_win", align_bytes=64, offset=0)
         word_win = keep.tile([P, T], U32, name="word_win", align_bytes=64)
-        h_raw = [
-            arena.tile([P, PACK, P], F32, name="h_raw0", align_bytes=64, offset=3072),
-            arena.tile([P, PACK, P], F32, name="h_raw1", align_bytes=64, offset=6144),
-            keep.tile([P, PACK, P], F32, name="h_raw2", align_bytes=64),
-            keep.tile([P, PACK, P], F32, name="h_raw3", align_bytes=64),
-        ]
+        h_raw = [arena.tile([P, PACK, P], F32, name="h_raw%d" % d, align_bytes=64, offset=4096 + 2048 * d) for d in range(TILES)]
 
-        nc.vector.memset(scale_win[:].bitcast(I32), 0)
-        nc.vector.memset(calib_win[0 : P - 2, :], 0.0)
+        scale_words = scale_win[:].bitcast(I32)
+        odd_words = scale_odd[:].bitcast(I32)
+        nc.vector.memset(scale_words[32:64], 0)
+        nc.vector.memset(scale_words[96:128], 0)
+        nc.vector.memset(calib_win[0 : P - 2, 16:T], 0.0)
 
         h_rows = hT.rearrange("(p j) t -> p j t", j=PACK)
+        scale_rows = x_scales[0].bitcast(I32).rearrange("(h q r) c -> q h r c", h=2, q=2)
         nc.sync.dma_start(offsets[:], offs)
+        nc.scalar.dma_start(odd_words, scale_rows[1].rearrange("h r c -> r h c"))
+        nc.sync.dma_start(scale_words[0:32], scale_rows[0, 0].unsqueeze(0).to_broadcast([8, 4, T // 4]))
         nc.scalar.dma_start(calib_win[P - 2 : P - 1, :], gain[0:1, :])
+        nc.sync.dma_start(scale_words[64:96], scale_rows[0, 1].unsqueeze(0).to_broadcast([8, 4, T // 4]))
         nc.sync.dma_start(calib_win[P - 1 : P, :], shift[0:1, :])
-
-        def load_scales(queue, q):
-            queue.dma_start(scale_win[32 * q : 32 * q + 4, :].bitcast(I32), x_scales[0, 4 * q : 4 * q + 4, :].bitcast(I32))
-
-        load_scales(nc.scalar, 0)
-        load_scales(nc.scalar, 1)
         nc.sync.dma_start(word_win[:].bitcast(I32), x_words[0].rearrange("p n t -> p (n t)").bitcast(I32))
-        nc.sync.dma_start(h_raw[0][:], h_rows[:, :, 0:P])
-        load_scales(nc.sync, 2)
-        load_scales(nc.sync, 3)
-        for d in range(1, 4):
+        for d in range(TILES):
             nc.sync.dma_start(h_raw[d][:], h_rows[:, :, d * P : (d + 1) * P])
+
+        nc.scalar.activation(calib_win[0 : P - 2, 0:16], calib_win[0 : P - 2, 16:32], ACT.Identity)
 
         ident = keep.tile([P, P], F32, name="ident")
         make_identity(nc, ident[:])
 
-        calib = arena.tile([P, S], F32, name="calib", align_bytes=64, offset=1024)
-        nc.vector.tensor_copy(calib[:], calib_win[:].indirect(offsets[:]))
+        nc.vector.tensor_copy(scale_words[32:36], odd_words[:, 0, :])
+        nc.vector.tensor_copy(scale_words[96:100], odd_words[:, 1, :])
+        x_scl = keep.tile([P, S], U8, name="x_scl", align_bytes=64)
+        nc.vector.tensor_copy(x_scl[:], scale_win[:].indirect(offsets[:]))
+        x_codes = keep.tile([P, S], U32, name="x_codes", align_bytes=64)
+        nc.vector.tensor_copy(x_codes[:], word_win[:].indirect(offsets[:]))
 
+        calib = arena.tile([P, S], F32, name="calib", align_bytes=64, offset=16384)
+        for h in range(2):
+            nc.scalar.activation(calib[:, 256 * h : 256 * h + 256], calib_win[:].indirect(offsets[:, 16 * h : 16 * h + 16]), ACT.Copy)
         calib_ps = psum.tile([P, CHUNKS, P], F32, name="calib_ps", tag="bank7")
         for c in range(CHUNKS):
             nc.tensor.transpose(calib_ps[:, c, :], calib[:, c * P : (c + 1) * P], ident[:])
@@ -74,137 +77,108 @@ def tile_picked_zplatt_soft_p_kernel(tc, x_words, x_scales, hT, gain, shift, off
         def scalar_cast(dst, src):
             nc.scalar.activation(dst, src, ACT.Identity)
 
-        def interleave(grouped, d, copy):
+        spare = 4096 + 2048 * TILES
+        bf_at = [0, 1024, 1024, spare]
+        code_at = [spare, spare + 1024, spare + 1536, spare + 2048]
+        h_bf = [arena.tile([P, P, PACK], BF16, name="h_bf%d" % d, align_bytes=64, offset=bf_at[d]) for d in range(TILES)]
+        h_codes = [arena.tile([P, P], U32, name="h_codes%d" % d, align_bytes=64, offset=code_at[d]) for d in range(TILES)]
+        h_scl = [arena.tile([P, P], U8, name="h_scl%d" % d, align_bytes=64, offset=17408 + P * d) for d in range(TILES)]
+
+        def interleave(d, copy):
             copy(
-                grouped.rearrange("p (c i) t -> p c t i", i=4),
+                h_bf[d][:].rearrange("p (c i) t -> p c t i", i=4),
                 h_raw[d][:].rearrange("p t (c i) -> p c t i", i=4),
             )
 
-        def quantize(grouped, h, docs):
+        def quantize(d):
             nc.vector.quantize_mx(
-                out=h_codes[h][:, docs].bitcast(FP8X4),
-                scales=h_scl[h][:, docs],
-                in_=grouped.rearrange("p w t -> p (w t)"),
+                out=h_codes[d][:].bitcast(FP8X4),
+                scales=h_scl[d][:],
+                in_=h_bf[d][:].rearrange("p w t -> p (w t)"),
             )
 
-        first, second, both = slice(0, P), slice(P, HALF), slice(0, HALF)
-        h_codes = [
-            keep.tile([P, HALF], U32, name="h_codes0", align_bytes=64),
-            keep.tile([P, HALF], U32, name="h_codes1", align_bytes=64),
-        ]
-        h_scl = [arena.tile([P, HALF], U8, name="h_scl%d" % h, align_bytes=64, offset=1088 + 256 * h) for h in range(2)]
+        zt_at = [20480 + 2048 * d for d in range(TILES)]
+        zt = [arena.tile([P, CHUNKS, P], F32, name="z_t%d" % d, align_bytes=64, offset=zt_at[d]) for d in range(TILES)]
+        calib_col = arena.tile([P, CHUNKS, 2], F32, name="calib_col", align_bytes=64, offset=4096)
 
-        x_early = keep.tile([P, 3 * P], U32, name="x_early", align_bytes=64)
-        nc.vector.tensor_copy(x_early[:], word_win[:].indirect(offsets[:, 0:24]))
+        def products(d, banks):
+            y = [psum.tile([P, 2, P], F32, name="y%d_%d" % (d, b), tag="bank%d" % b) for b in banks]
+            for c in range(CHUNKS):
+                nc.tensor.matmul_mx(
+                    out=y[c // 2][:, c % 2, :],
+                    lhsT=x_codes[:, c * P : (c + 1) * P].bitcast(FP8X4),
+                    lhsT_scale=x_scl[:, c * P : (c + 1) * P],
+                    rhs=h_codes[d][:].bitcast(FP8X4),
+                    rhs_scale=h_scl[d][:],
+                    start=True,
+                    stop=True,
+                )
+            return y
 
-        x_scl = [keep.tile([P, HALF], U8, name="x_scl%d" % h, align_bytes=64) for h in range(2)]
-        for h in range(2):
-            nc.vector.tensor_copy(x_scl[h][:], scale_win[:].indirect(offsets[:, 16 * h : 16 * h + 16]))
+        def affines(d, y, on_scalar):
+            for c in range(CHUNKS):
+                slope, offset = calib_col[:, c, 0:1], calib_col[:, c, 1:2]
+                if c < on_scalar:
+                    nc.scalar.activation(zt[d][:, c, :], y[c // 2][:, c % 2, :], ACT.Identity, bias=offset, scale=slope)
+                else:
+                    nc.vector.tensor_scalar(zt[d][:, c, :], y[c // 2][:, c % 2, :], slope, offset, ALU.mult, ALU.add)
 
-        h_bf0 = arena.tile([P, P, PACK], BF16, name="h_bf0", align_bytes=64, offset=5120)
-        interleave(h_bf0[:], 0, scalar_cast)
-        quantize(h_bf0[:], 0, first)
-        x_late = arena.tile([P, P], U32, name="x_late", align_bytes=64, offset=2624)
-        nc.vector.tensor_copy(x_late[:], word_win[:].indirect(offsets[:, 24:32]))
-        x_codes = [x_early[:, c * P : (c + 1) * P] for c in range(3)] + [x_late[:]]
-
-        calib_col = arena.tile([P, CHUNKS, 2], F32, name="calib_col", align_bytes=64, offset=3584)
-        nc.scalar.copy(calib_col[:], calib_ps[:, :, P - 2 : P])
-
-        h_bf1 = arena.tile([P, P, PACK], BF16, name="h_bf1", align_bytes=64, offset=64)
-        interleave(h_bf1[:], 1, scalar_cast)
-        quantize(h_bf1[:], 0, second)
-
-        h_bf2 = arena.tile([P, P, PACK], BF16, name="h_bf2", align_bytes=64, offset=1600)
-        interleave(h_bf2[:], 2, scalar_cast)
-        h_bf3 = arena.tile([P, P, PACK], BF16, name="h_bf3", align_bytes=64, offset=5632)
-        interleave(h_bf3[:], 3, nc.vector.tensor_copy)
-        quantize(h_bf2[:], 1, first)
-        quantize(h_bf3[:], 1, second)
-
-        warm = psum.tile([P, 2, HALF], F32, name="warm", tag="bank7")
-
-        def spare_pass(i, codes, scales):
-            nc.tensor.matmul_mx(
-                out=warm[:, i, :],
-                lhsT=codes.bitcast(FP8X4),
-                lhsT_scale=scales,
-                rhs=x_early[:, 0:HALF].bitcast(FP8X4),
-                rhs_scale=x_scl[0][:],
-                start=True,
-                stop=True,
-            )
-
-        spare_pass(0, x_early[:, 0:P], x_scl[0][:, 0:P])
-        spare_pass(1, x_early[:, 0:P], x_scl[0][:, 0:P])
-
-        zt = [keep.tile([P, CHUNKS, HALF], F32, name="z_t%d" % h, align_bytes=64) for h in range(2)]
-
-        def product_banks(name, width, banks):
-            tiles = {b: psum.tile([P, banks.count(b), width], F32, name="%s_%d" % (name, b), tag="bank%d" % b) for b in set(banks)}
-            return [tiles[b][:, banks[:c].count(b), :] for c, b in enumerate(banks)]
-
-        def product(y, h, docs, c):
-            nc.tensor.matmul_mx(
-                out=y[c],
-                lhsT=x_codes[c].bitcast(FP8X4),
-                lhsT_scale=x_scl[c // 2][:, (c % 2) * P : (c % 2 + 1) * P],
-                rhs=h_codes[h][:, docs].bitcast(FP8X4),
-                rhs_scale=h_scl[h][:, docs],
-                start=True,
-                stop=True,
-            )
-
-        def affine(y, h, docs, c, on_vector):
-            slope, offset = calib_col[:, c, 0:1], calib_col[:, c, 1:2]
-            if on_vector:
-                nc.vector.tensor_scalar(zt[h][:, c, docs], y[c], slope, offset, ALU.mult, ALU.add)
-            else:
-                nc.scalar.activation(zt[h][:, c, docs], y[c], ACT.Identity, bias=offset, scale=slope)
-
-        def turn_and_max(d, bank):
-            h, u = divmod(d, 2)
+        def turn(d, bank):
             z = psum.tile([P, S], F32, name="z%d" % d, tag="bank%d" % bank)
             for c in range(CHUNKS):
-                nc.tensor.transpose(z[:, c * P : (c + 1) * P], zt[h][:, c, u * P : (u + 1) * P], ident[:])
+                nc.tensor.transpose(z[:, c * P : (c + 1) * P], zt[d][:, c, :], ident[:])
+            return z
+
+        def row_max(d, z):
             neg_max = keep.tile([P, 1], F32, name="neg_max%d" % d)
             nc.vector.tensor_reduce(neg_max[:], z[:], AX.X, ALU.max, negate=True)
-            return z, neg_max
+            return neg_max
 
-        def finish(d, z, neg_max):
+        def exponential(d, z, neg_max):
             total = keep.tile([P, 1], F32, name="total%d" % d)
-            inv = keep.tile([P, 1], F32, name="inv%d" % d)
             e = keep.tile([P, S], F32, name="e%d" % d)
             nc.scalar.activation(e[:], z[:], ACT.Exp, bias=neg_max[:], scale=1.0, accum_out=total[:])
+            return e, total
+
+        def finish(d, e, total):
+            inv = arena.tile([P, 1], F32, name="inv%d" % d, align_bytes=64, offset=zt_at[min(d + 1, TILES - 1)] + 64 * (d // 3) + 1536)
             nc.vector.reciprocal(inv[:], total[:])
             prob = keep.tile([P, S], F32, name="prob%d" % d)
-            if d < 1:
+            if d < 2:
                 nc.gpsimd.tensor_scalar(prob[:], e[:], inv[:], 0.0, ALU.mult, ALU.add)
             else:
                 nc.vector.tensor_scalar(prob[:], e[:], inv[:], None, ALU.mult)
             nc.sync.dma_start(out[d * P : (d + 1) * P, :], prob[:])
 
-        y_first = product_banks("y_first", P, [0, 0, 6, 1])
-        y_second = product_banks("y_second", P, [2, 2, 3, 4])
-        for c in range(CHUNKS):
-            product(y_first, 0, first, c)
-        for c in range(CHUNKS):
-            product(y_second, 0, second, c)
-        for c in range(CHUNKS):
-            affine(y_first, 0, first, c, False)
-        for c in range(CHUNKS):
-            affine(y_second, 0, second, c, c < 2)
-        tile0 = turn_and_max(0, 5)
-        y_third = product_banks("y_third", P, [1, 1, 0, 0])
-        y_fourth = product_banks("y_fourth", P, [3, 3, 4, 4])
-        for c in range(CHUNKS):
-            product(y_third, 1, first, c)
-        for c in range(CHUNKS):
-            product(y_fourth, 1, second, c)
-        for c in range(CHUNKS):
-            affine(y_third, 1, first, c, c >= 2)
-        for c in range(CHUNKS):
-            affine(y_fourth, 1, second, c, c >= 2)
-        finish(0, *tile0)
-        for d, bank in ((1, 7), (2, 6), (3, 2)):
-            finish(d, *turn_and_max(d, bank))
+        interleave(0, scalar_cast)
+        quantize(0)
+        interleave(1, scalar_cast)
+        quantize(1)
+        nc.scalar.copy(calib_col[:], calib_ps[:, :, P - 2 : P])
+        interleave(2, nc.vector.tensor_copy)
+        y0 = products(0, [0, 1])
+        y1 = products(1, [2, 3])
+        affines(0, y0, 2)
+        quantize(2)
+        interleave(3, nc.vector.tensor_copy)
+        quantize(3)
+        affines(1, y1, 4)
+        z0 = turn(0, 4)
+        m0 = row_max(0, z0)
+        y2 = products(2, [0, 1])
+        affines(2, y2, 2)
+        e0 = exponential(0, z0, m0)
+        z1 = turn(1, 5)
+        m1 = row_max(1, z1)
+        y3 = products(3, [2, 3])
+        affines(3, y3, 2)
+        finish(0, *e0)
+        e1 = exponential(1, z1, m1)
+        z2 = turn(2, 6)
+        m2 = row_max(2, z2)
+        finish(1, *e1)
+        e2 = exponential(2, z2, m2)
+        z3 = turn(3, 7)
+        m3 = row_max(3, z3)
+        finish(2, *e2)
+        finish(3, *exponential(3, z3, m3))

@@ -39,18 +39,17 @@ def tile_picked_zplatt_soft_p_kernel(tc, x_words, x_scales, hT, gain, shift, off
 
         scale_words = scale_win[:].bitcast(I32)
         odd_words = scale_odd[:].bitcast(I32)
-        nc.vector.memset(scale_words[32:64], 0)
-        nc.vector.memset(scale_words[96:128], 0)
+        nc.vector.memset(scale_words, 0)
         nc.vector.memset(calib_win[0 : P - 2, 16:T], 0.0)
 
         h_rows = hT.rearrange("(p j) t -> p j t", j=PACK)
         scale_rows = x_scales[0].bitcast(I32).rearrange("(h q r) c -> q h r c", h=2, q=2)
         nc.sync.dma_start(offsets[:], offs)
         nc.scalar.dma_start(odd_words, scale_rows[1].rearrange("h r c -> r h c"))
-        nc.sync.dma_start(scale_words[0:32], scale_rows[0, 0].unsqueeze(0).to_broadcast([8, 4, T // 4]))
-        nc.scalar.dma_start(calib_win[P - 2 : P - 1, :], gain[0:1, :])
-        nc.sync.dma_start(scale_words[64:96], scale_rows[0, 1].unsqueeze(0).to_broadcast([8, 4, T // 4]))
+        nc.sync.dma_start(calib_win[P - 2 : P - 1, :], gain[0:1, :])
         nc.sync.dma_start(calib_win[P - 1 : P, :], shift[0:1, :])
+        nc.sync.dma_start(scale_words[0:4], scale_rows[0, 0])
+        nc.sync.dma_start(scale_words[64:68], scale_rows[0, 1])
         nc.sync.dma_start(word_win[:].bitcast(I32), x_words[0].rearrange("p n t -> p (n t)").bitcast(I32))
         for d in range(TILES):
             nc.sync.dma_start(h_raw[d][:], h_rows[:, :, d * P : (d + 1) * P])

@@ -22,6 +22,8 @@ TILES = J // P
 FLOPS = 2 * K * S * J
 BYTES = K * T + 16 * T + 4 * K * J + 2 * 4 * T + 2 * S + 4 * J * S
 
+HALF = S // 2
+
 
 def tile_picked_zplatt_soft_p_kernel(tc, x_words, x_scales, hT, gain, shift, offs, out):
     nc = tc.nc
@@ -30,28 +32,36 @@ def tile_picked_zplatt_soft_p_kernel(tc, x_words, x_scales, hT, gain, shift, off
         arena = ctx.enter_context(tc.tile_pool(name="arena", bufs=1))
         psum = ctx.enter_context(tc.psum_pool(name="psum", bufs=1))
 
-        offsets = keep.tile([P, S // 16], U16, name="offsets")
-        scale_win = keep.tile([P, T], U8, name="scale_win", align_bytes=64)
-        scale_odd = keep.tile([4, 2, T], U8, name="scale_odd", align_bytes=64)
-        calib_win = arena.tile([P, T], F32, name="calib_win", align_bytes=64, offset=0)
-        word_win = keep.tile([P, T], U32, name="word_win", align_bytes=64)
-        h_raw = [arena.tile([P, PACK, P], F32, name="h_raw%d" % d, align_bytes=64, offset=4096 + 2048 * d) for d in range(TILES)]
+        calib_win_at, calib_at, h_raw1_at, h_bf1_at, late_col_at = 0, 4096, 6144, 8192, 11264
 
-        scale_words = scale_win[:].bitcast(I32)
-        odd_words = scale_odd[:].bitcast(I32)
-        nc.vector.memset(scale_words, 0)
+        def placed(shape, dtype, name, offset):
+            return arena.tile(shape, dtype, name=name, align_bytes=64, offset=offset)
+
+        def kept(shape, dtype, name):
+            return keep.tile(shape, dtype, name=name, align_bytes=64)
+
+        offsets = keep.tile([P, S // 16], U16, name="offsets")
+        scale_win = kept([P, T], U8, "scale_win")
+        calib_win = placed([P, T], F32, "calib_win", calib_win_at)
+        word_win = kept([P, T], U32, "word_win")
+        h_raw = [placed([P, PACK, P], F32, "h_raw1", h_raw1_at) if d == 1 else kept([P, PACK, P], F32, "h_raw%d" % d) for d in range(TILES)]
+
+        nc.vector.memset(scale_win[:].bitcast(I32), 0)
         nc.vector.memset(calib_win[0 : P - 2, 16:T], 0.0)
 
         h_rows = hT.rearrange("(p j) t -> p j t", j=PACK)
-        scale_rows = x_scales[0].bitcast(I32).rearrange("(h q r) c -> q h r c", h=2, q=2)
+
+        def load_scales(q):
+            nc.sync.dma_start(scale_win[32 * q : 32 * q + 4, :].bitcast(I32), x_scales[0, 4 * q : 4 * q + 4, :].bitcast(I32))
+
         nc.sync.dma_start(offsets[:], offs)
-        nc.scalar.dma_start(odd_words, scale_rows[1].rearrange("h r c -> r h c"))
-        nc.sync.dma_start(calib_win[P - 2 : P - 1, :], gain[0:1, :])
+        nc.scalar.dma_start(calib_win[P - 2 : P - 1, :], gain[0:1, :])
         nc.sync.dma_start(calib_win[P - 1 : P, :], shift[0:1, :])
-        nc.sync.dma_start(scale_words[0:4], scale_rows[0, 0])
-        nc.sync.dma_start(scale_words[64:68], scale_rows[0, 1])
         nc.sync.dma_start(word_win[:].bitcast(I32), x_words[0].rearrange("p n t -> p (n t)").bitcast(I32))
-        for d in range(TILES):
+        nc.sync.dma_start(h_raw[0][:], h_rows[:, :, 0:P])
+        for q in range(4):
+            load_scales(q)
+        for d in range(1, TILES):
             nc.sync.dma_start(h_raw[d][:], h_rows[:, :, d * P : (d + 1) * P])
 
         nc.scalar.activation(calib_win[0 : P - 2, 0:16], calib_win[0 : P - 2, 16:32], ACT.Identity)
@@ -59,46 +69,37 @@ def tile_picked_zplatt_soft_p_kernel(tc, x_words, x_scales, hT, gain, shift, off
         ident = keep.tile([P, P], F32, name="ident")
         make_identity(nc, ident[:])
 
-        nc.vector.tensor_copy(scale_words[32:36], odd_words[:, 0, :])
-        nc.vector.tensor_copy(scale_words[96:100], odd_words[:, 1, :])
-        x_scl = keep.tile([P, S], U8, name="x_scl", align_bytes=64)
-        nc.vector.tensor_copy(x_scl[:], scale_win[:].indirect(offsets[:]))
-        x_codes = keep.tile([P, S], U32, name="x_codes", align_bytes=64)
-        nc.vector.tensor_copy(x_codes[:], word_win[:].indirect(offsets[:]))
-
-        calib = arena.tile([P, S], F32, name="calib", align_bytes=64, offset=16384)
+        calib = placed([P, S], F32, "calib", calib_at)
         for h in range(2):
-            nc.scalar.activation(calib[:, 256 * h : 256 * h + 256], calib_win[:].indirect(offsets[:, 16 * h : 16 * h + 16]), ACT.Copy)
+            nc.scalar.activation(calib[:, HALF * h : HALF * (h + 1)], calib_win[:].indirect(offsets[:, 16 * h : 16 * h + 16]), ACT.Copy)
         calib_ps = psum.tile([P, CHUNKS, P], F32, name="calib_ps", tag="bank7")
         for c in range(CHUNKS):
             nc.tensor.transpose(calib_ps[:, c, :], calib[:, c * P : (c + 1) * P], ident[:])
 
+        x_codes = kept([P, S], U32, "x_codes")
+        nc.vector.tensor_copy(x_codes[:], word_win[:].indirect(offsets[:]))
+        x_scl = [kept([P, HALF], U8, "x_scl0"), placed([P, HALF], U8, "x_scl1", calib_at + 1024)]
+
+        def gather_scales(h):
+            nc.vector.tensor_copy(x_scl[h][:], scale_win[:].indirect(offsets[:, 16 * h : 16 * h + 16]))
+
         def scalar_cast(dst, src):
             nc.scalar.activation(dst, src, ACT.Identity)
 
-        spare = 4096 + 2048 * TILES
-        bf_at = [0, 1024, 1024, spare]
-        code_at = [spare, spare + 1024, spare + 1536, spare + 2048]
-        h_bf = [arena.tile([P, P, PACK], BF16, name="h_bf%d" % d, align_bytes=64, offset=bf_at[d]) for d in range(TILES)]
-        h_codes = [arena.tile([P, P], U32, name="h_codes%d" % d, align_bytes=64, offset=code_at[d]) for d in range(TILES)]
-        h_scl = [arena.tile([P, P], U8, name="h_scl%d" % d, align_bytes=64, offset=17408 + P * d) for d in range(TILES)]
+        h_bf = [
+            placed([P, P, PACK], BF16, "h_bf0", calib_win_at)[:],
+            placed([P, 3 * P, PACK], BF16, "h_bf1", h_bf1_at)[:, 0:P, :],
+            placed([P, P, PACK], BF16, "h_bf2", h_bf1_at)[:],
+            placed([P, P, PACK], BF16, "h_bf3", h_bf1_at + 2048)[:],
+        ]
+        h_codes = [kept([P, P], U32, "h_codes%d" % d) for d in range(TILES)]
+        h_scl = [placed([P, P], U8, "h_scl%d" % d, calib_at + P * d) for d in range(TILES)]
 
         def interleave(d, copy):
-            copy(
-                h_bf[d][:].rearrange("p (c i) t -> p c t i", i=4),
-                h_raw[d][:].rearrange("p t (c i) -> p c t i", i=4),
-            )
+            copy(h_bf[d].rearrange("p (c i) t -> p c t i", i=4), h_raw[d][:].rearrange("p t (c i) -> p c t i", i=4))
 
         def quantize(d):
-            nc.vector.quantize_mx(
-                out=h_codes[d][:].bitcast(FP8X4),
-                scales=h_scl[d][:],
-                in_=h_bf[d][:].rearrange("p w t -> p (w t)"),
-            )
-
-        zt_at = [20480 + 2048 * d for d in range(TILES)]
-        zt = [arena.tile([P, CHUNKS, P], F32, name="z_t%d" % d, align_bytes=64, offset=zt_at[d]) for d in range(TILES)]
-        calib_col = arena.tile([P, CHUNKS, 2], F32, name="calib_col", align_bytes=64, offset=4096)
+            nc.vector.quantize_mx(out=h_codes[d][:].bitcast(FP8X4), scales=h_scl[d][:], in_=h_bf[d].rearrange("p w t -> p (w t)"))
 
         def products(d, banks):
             y = [psum.tile([P, 2, P], F32, name="y%d_%d" % (d, b), tag="bank%d" % b) for b in banks]
@@ -106,7 +107,7 @@ def tile_picked_zplatt_soft_p_kernel(tc, x_words, x_scales, hT, gain, shift, off
                 nc.tensor.matmul_mx(
                     out=y[c // 2][:, c % 2, :],
                     lhsT=x_codes[:, c * P : (c + 1) * P].bitcast(FP8X4),
-                    lhsT_scale=x_scl[:, c * P : (c + 1) * P],
+                    lhsT_scale=x_scl[c // 2][:, (c % 2) * P : (c % 2 + 1) * P],
                     rhs=h_codes[d][:].bitcast(FP8X4),
                     rhs_scale=h_scl[d][:],
                     start=True,
@@ -114,70 +115,76 @@ def tile_picked_zplatt_soft_p_kernel(tc, x_words, x_scales, hT, gain, shift, off
                 )
             return y
 
-        def affines(d, y, on_scalar):
-            for c in range(CHUNKS):
-                slope, offset = calib_col[:, c, 0:1], calib_col[:, c, 1:2]
-                if c < on_scalar:
-                    nc.scalar.activation(zt[d][:, c, :], y[c // 2][:, c % 2, :], ACT.Identity, bias=offset, scale=slope)
-                else:
-                    nc.vector.tensor_scalar(zt[d][:, c, :], y[c // 2][:, c % 2, :], slope, offset, ALU.mult, ALU.add)
+        calib_col = kept([P, CHUNKS, 2], F32, "calib_col")
+        late_col = placed([P, 2, 2], F32, "late_col", late_col_at)
+        zt_at = {(0, 0): h_raw1_at, (0, 1): h_bf1_at + 1024, (1, 0): h_bf1_at, (3, 0): late_col_at}
 
-        def turn(d, bank):
+        def affines(d, y):
+            zt = [placed([P, 2, P], F32, "zt%d_%d" % (d, h), zt_at[d, h]) if (d, h) in zt_at else kept([P, 2, P], F32, "zt%d_%d" % (d, h)) for h in range(2)]
+            for c in range(2):
+                nc.scalar.activation(zt[0][:, c, :], y[0][:, c, :], ACT.Identity, bias=calib_col[:, c, 1:2], scale=calib_col[:, c, 0:1])
+            col = late_col[:] if d == 2 else calib_col[:, 2:4, :]
+            for c in range(2):
+                nc.vector.tensor_scalar(zt[1][:, c, :], y[1][:, c, :], col[:, c, 0:1], col[:, c, 1:2], ALU.mult, ALU.add)
+            return zt
+
+        def turn(d, zt, bank):
             z = psum.tile([P, S], F32, name="z%d" % d, tag="bank%d" % bank)
             for c in range(CHUNKS):
-                nc.tensor.transpose(z[:, c * P : (c + 1) * P], zt[d][:, c, :], ident[:])
+                nc.tensor.transpose(z[:, c * P : (c + 1) * P], zt[c // 2][:, c % 2, :], ident[:])
             return z
 
         def row_max(d, z):
-            neg_max = keep.tile([P, 1], F32, name="neg_max%d" % d)
+            neg_max = kept([P, 1], F32, "neg_max%d" % d)
             nc.vector.tensor_reduce(neg_max[:], z[:], AX.X, ALU.max, negate=True)
             return neg_max
 
         def exponential(d, z, neg_max):
-            total = keep.tile([P, 1], F32, name="total%d" % d)
-            e = keep.tile([P, S], F32, name="e%d" % d)
+            total = kept([P, 1], F32, "total%d" % d)
+            e = kept([P, S], F32, "e%d" % d)
             nc.scalar.activation(e[:], z[:], ACT.Exp, bias=neg_max[:], scale=1.0, accum_out=total[:])
             return e, total
 
         def finish(d, e, total):
-            inv = arena.tile([P, 1], F32, name="inv%d" % d, align_bytes=64, offset=zt_at[min(d + 1, TILES - 1)] + 64 * (d // 3) + 1536)
+            inv = kept([P, 1], F32, "inv%d" % d)
             nc.vector.reciprocal(inv[:], total[:])
-            prob = keep.tile([P, S], F32, name="prob%d" % d)
+            prob = kept([P, S], F32, "prob%d" % d)
             if d < 2:
                 nc.gpsimd.tensor_scalar(prob[:], e[:], inv[:], 0.0, ALU.mult, ALU.add)
             else:
                 nc.vector.tensor_scalar(prob[:], e[:], inv[:], None, ALU.mult)
             nc.sync.dma_start(out[d * P : (d + 1) * P, :], prob[:])
 
+        gather_scales(0)
         interleave(0, scalar_cast)
         quantize(0)
+        gather_scales(1)
+        nc.scalar.copy(calib_col[:], calib_ps[:, :, P - 2 : P])
+        nc.scalar.copy(late_col[:], calib_ps[:, 2:4, P - 2 : P])
         interleave(1, scalar_cast)
         quantize(1)
-        nc.scalar.copy(calib_col[:], calib_ps[:, :, P - 2 : P])
         interleave(2, nc.vector.tensor_copy)
         y0 = products(0, [0, 1])
         y1 = products(1, [2, 3])
-        affines(0, y0, 2)
+        zt0 = affines(0, y0)
         quantize(2)
-        interleave(3, nc.vector.tensor_copy)
+        interleave(3, scalar_cast)
+        zt1 = affines(1, y1)
         quantize(3)
-        affines(1, y1, 4)
-        z0 = turn(0, 4)
+        z0 = turn(0, zt0, 4)
         m0 = row_max(0, z0)
-        y2 = products(2, [0, 1])
-        affines(2, y2, 2)
+        zt2 = affines(2, products(2, [0, 1]))
         e0 = exponential(0, z0, m0)
-        z1 = turn(1, 5)
+        z1 = turn(1, zt1, 5)
         m1 = row_max(1, z1)
-        y3 = products(3, [2, 3])
-        affines(3, y3, 2)
+        zt3 = affines(3, products(3, [2, 3]))
         finish(0, *e0)
         e1 = exponential(1, z1, m1)
-        z2 = turn(2, 6)
+        z2 = turn(2, zt2, 6)
         m2 = row_max(2, z2)
         finish(1, *e1)
         e2 = exponential(2, z2, m2)
-        z3 = turn(3, 7)
+        z3 = turn(3, zt3, 7)
         m3 = row_max(3, z3)
         finish(2, *e2)
         finish(3, *exponential(3, z3, m3))

@@ -101,6 +101,18 @@ def tile_picked_zplatt_soft_p_kernel(tc, x_words, x_scales, hT, gain, shift, off
         def quantize(d):
             nc.vector.quantize_mx(out=h_codes[d][:].bitcast(FP8X4), scales=h_scl[d][:], in_=h_bf[d].rearrange("p w t -> p (w t)"))
 
+        def warm_up():
+            warm = psum.tile([P, HALF], F32, name="warm", tag="bank6")
+            nc.tensor.matmul_mx(
+                out=warm[:],
+                lhsT=h_codes[0][:].bitcast(FP8X4),
+                lhsT_scale=h_scl[0][:],
+                rhs=x_codes[:, 0:HALF].bitcast(FP8X4),
+                rhs_scale=x_scl[0][:],
+                start=True,
+                stop=True,
+            )
+
         def products(d, banks):
             y = [psum.tile([P, 2, P], F32, name="y%d_%d" % (d, b), tag="bank%d" % b) for b in banks]
             for c in range(CHUNKS):
@@ -113,6 +125,8 @@ def tile_picked_zplatt_soft_p_kernel(tc, x_words, x_scales, hT, gain, shift, off
                     start=True,
                     stop=True,
                 )
+                if d == 0 and c == 1:
+                    warm_up()
             return y
 
         calib_col = kept([P, CHUNKS, 2], F32, "calib_col")

@@ -144,7 +144,7 @@ def tile_picked_zplatt_soft_p_kernel(tc, x_words, x_scales, hT, gain, shift, off
 
         def turn(d, zt, bank):
             z = psum.tile([P, S], F32, name="z%d" % d, tag="bank%d" % bank)
-            for c in range(CHUNKS):
+            for c in (0, 2, 1, 3) if d > 1 else range(CHUNKS):
                 nc.tensor.transpose(z[:, c * P : (c + 1) * P], zt[c // 2][:, c % 2, :], ident[:])
             return z
 
@@ -159,11 +159,14 @@ def tile_picked_zplatt_soft_p_kernel(tc, x_words, x_scales, hT, gain, shift, off
             nc.scalar.activation(e[:], z[:], ACT.Exp, bias=neg_max[:], scale=1.0, accum_out=total[:])
             return e, total
 
-        def finish(d, e, total):
+        def invert(d, total):
             inv = kept([P, 1], F32, "inv%d" % d)
             nc.vector.reciprocal(inv[:], total[:])
+            return inv
+
+        def finish(d, e, inv):
             prob = kept([P, S], F32, "prob%d" % d)
-            if d < 2:
+            if d < 1:
                 nc.gpsimd.tensor_scalar(prob[:], e[:], inv[:], 0.0, ALU.mult, ALU.add)
             else:
                 nc.vector.tensor_scalar(prob[:], e[:], inv[:], None, ALU.mult)
@@ -188,17 +191,19 @@ def tile_picked_zplatt_soft_p_kernel(tc, x_words, x_scales, hT, gain, shift, off
         z0 = turn(0, zt0, 4)
         m0 = row_max(0, z0)
         zt2 = affines(2, products(2, [0, 1]))
-        e0 = exponential(0, z0, m0)
+        e0, total0 = exponential(0, z0, m0)
         z1 = turn(1, zt1, 5)
         m1 = row_max(1, z1)
         zt3 = affines(3, products(3, [2, 3]))
-        finish(0, *e0)
-        e1 = exponential(1, z1, m1)
+        finish(0, e0, invert(0, total0))
+        e1, total1 = exponential(1, z1, m1)
         z2 = turn(2, zt2, 6)
         m2 = row_max(2, z2)
-        finish(1, *e1)
-        e2 = exponential(2, z2, m2)
+        inv1 = invert(1, total1)
+        e2, total2 = exponential(2, z2, m2)
         z3 = turn(3, zt3, 7)
         m3 = row_max(3, z3)
-        finish(2, *e2)
-        finish(3, *exponential(3, z3, m3))
+        finish(1, e1, inv1)
+        finish(2, e2, invert(2, total2))
+        e3, total3 = exponential(3, z3, m3)
+        finish(3, e3, invert(3, total3))

@@ -70,8 +70,8 @@ def tile_picked_zplatt_soft_p_kernel(tc, x_words, x_scales, hT, gain, shift, off
         make_identity(nc, ident[:])
 
         calib = placed([P, S], F32, "calib", calib_at)
-        for h in range(2):
-            nc.scalar.activation(calib[:, HALF * h : HALF * (h + 1)], calib_win[:].indirect(offsets[:, 16 * h : 16 * h + 16]), ACT.Copy)
+        nc.vector.tensor_copy(calib[:, 0:HALF], calib_win[:].indirect(offsets[:, 0:16]))
+        nc.scalar.activation(calib[:, HALF:S], calib_win[:].indirect(offsets[:, 16:32]), ACT.Copy)
         calib_ps = psum.tile([P, CHUNKS, P], F32, name="calib_ps", tag="bank7")
         for c in range(CHUNKS):
             nc.tensor.transpose(calib_ps[:, c, :], calib[:, c * P : (c + 1) * P], ident[:])

from contextlib import ExitStack

import concourse.mybir as mybir
from concourse.masks import make_identity

F32 = mybir.dt.float32
BF16 = mybir.dt.bfloat16
I32 = mybir.dt.int32
U32 = mybir.dt.uint32
U16 = mybir.dt.uint16
U8 = mybir.dt.uint8
FP8X4 = mybir.dt.float8_e4m3fn_x4
ALU = mybir.AluOpType
ACT = mybir.ActivationFunctionType
AX = mybir.AxisListType

P = 128
PACK = 4
K, T, S, J = 512, 1024, 512, 512
CHUNKS = S // P
TILES = J // P
FLOPS = 2 * K * S * J
BYTES = K * T + 16 * T + 4 * K * J + 2 * 4 * T + 2 * S + 4 * J * S

HALF = S // 2


def tile_picked_zplatt_soft_p_kernel(tc, x_words, x_scales, hT, gain, shift, offs, out):
    nc = tc.nc
    with ExitStack() as ctx:
        keep = ctx.enter_context(tc.tile_pool(name="keep", bufs=1))
        arena = ctx.enter_context(tc.tile_pool(name="arena", bufs=1))
        psum = ctx.enter_context(tc.psum_pool(name="psum", bufs=1))

        calib_win_at, calib_at, h_raw1_at, h_bf1_at, late_col_at = 0, 4096, 6144, 8192, 11264

        def placed(shape, dtype, name, offset):
            return arena.tile(shape, dtype, name=name, align_bytes=64, offset=offset)

        def kept(shape, dtype, name):
            return keep.tile(shape, dtype, name=name, align_bytes=64)

        offsets = keep.tile([P, S // 16], U16, name="offsets")
        scale_win = kept([P, T], U8, "scale_win")
        calib_win = placed([P, T], F32, "calib_win", calib_win_at)
        word_win = kept([P, T], U32, "word_win")
        h_raw = [placed([P, PACK, P], F32, "h_raw1", h_raw1_at) if d == 1 else kept([P, PACK, P], F32, "h_raw%d" % d) for d in range(TILES)]

        nc.vector.memset(scale_win[:].bitcast(I32), 0)
        nc.vector.memset(calib_win[0 : P - 2, 16:T], 0.0)

        h_rows = hT.rearrange("(p j) t -> p j t", j=PACK)

        def load_scales(q):
            nc.sync.dma_start(scale_win[32 * q : 32 * q + 4, :].bitcast(I32), x_scales[0, 4 * q : 4 * q + 4, :].bitcast(I32))

        nc.sync.dma_start(offsets[:], offs)
        nc.scalar.dma_start(calib_win[P - 2 : P - 1, :], gain[0:1, :])
        nc.sync.dma_start(calib_win[P - 1 : P, :], shift[0:1, :])
        nc.sync.dma_start(word_win[:].bitcast(I32), x_words[0].rearrange("p n t -> p (n t)").bitcast(I32))
        nc.sync.dma_start(h_raw[0][:], h_rows[:, :, 0:P])
        for q in range(4):
            load_scales(q)
        for d in range(1, TILES):
            nc.sync.dma_start(h_raw[d][:], h_rows[:, :, d * P : (d + 1) * P])

        nc.scalar.activation(calib_win[0 : P - 2, 0:16], calib_win[0 : P - 2, 16:32], ACT.Identity)

        ident = keep.tile([P, P], F32, name="ident")
        make_identity(nc, ident[:])

        calib = placed([P, S], F32, "calib", calib_at)
        nc.vector.tensor_copy(calib[:, 0:HALF], calib_win[:].indirect(offsets[:, 0:16]))
        nc.scalar.activation(calib[:, HALF:S], calib_win[:].indirect(offsets[:, 16:32]), ACT.Copy)
        calib_ps = psum.tile([P, CHUNKS, P], F32, name="calib_ps", tag="bank7")
        for c in range(CHUNKS):
            nc.tensor.transpose(calib_ps[:, c, :], calib[:, c * P : (c + 1) * P], ident[:])

        x_codes = kept([P, S], U32, "x_codes")
        nc.vector.tensor_copy(x_codes[:], word_win[:].indirect(offsets[:]))
        x_scl = [kept([P, HALF], U8, "x_scl0"), placed([P, HALF], U8, "x_scl1", calib_at + 1024)]

        def gather_scales(h):
            nc.vector.tensor_copy(x_scl[h][:], scale_win[:].indirect(offsets[:, 16 * h : 16 * h + 16]))

        def scalar_cast(dst, src):
            nc.scalar.activation(dst, src, ACT.Identity)

        h_bf = [
            placed([P, P, PACK], BF16, "h_bf0", calib_win_at)[:],
            placed([P, 3 * P, PACK], BF16, "h_bf1", h_bf1_at)[:, 0:P, :],
            placed([P, P, PACK], BF16, "h_bf2", h_bf1_at)[:],
            placed([P, P, PACK], BF16, "h_bf3", h_bf1_at + 2048)[:],
        ]
        h_codes = [kept([P, P], U32, "h_codes%d" % d) for d in range(TILES)]
        h_scl = [placed([P, P], U8, "h_scl%d" % d, calib_at + P * d) for d in range(TILES)]

        def interleave(d, copy):
            copy(h_bf[d].rearrange("p (c i) t -> p c t i", i=4), h_raw[d][:].rearrange("p t (c i) -> p c t i", i=4))

        def quantize(d):
            nc.vector.quantize_mx(out=h_codes[d][:].bitcast(FP8X4), scales=h_scl[d][:], in_=h_bf[d].rearrange("p w t -> p (w t)"))

        def warm_up():
            warm = psum.tile([P, HALF], F32, name="warm", tag="bank6")
            nc.tensor.matmul_mx(
                out=warm[:],
                lhsT=h_codes[0][:].bitcast(FP8X4),
                lhsT_scale=h_scl[0][:],
                rhs=x_codes[:, 0:HALF].bitcast(FP8X4),
                rhs_scale=x_scl[0][:],
                start=True,
                stop=True,
            )

        def products(d, banks):
            y = [psum.tile([P, 2, P], F32, name="y%d_%d" % (d, b), tag="bank%d" % b) for b in banks]
            for c in range(CHUNKS):
                nc.tensor.matmul_mx(
                    out=y[c // 2][:, c % 2, :],
                    lhsT=x_codes[:, c * P : (c + 1) * P].bitcast(FP8X4),
                    lhsT_scale=x_scl[c // 2][:, (c % 2) * P : (c % 2 + 1) * P],
                    rhs=h_codes[d][:].bitcast(FP8X4),
                    rhs_scale=h_scl[d][:],
                    start=True,
                    stop=True,
                )
                if d == 0 and c == 1:
                    warm_up()
            return y

        calib_col = kept([P, CHUNKS, 2], F32, "calib_col")
        late_col = placed([P, 2, 2], F32, "late_col", late_col_at)
        zt_at = {(0, 0): h_raw1_at, (0, 1): h_bf1_at + 1024, (1, 0): h_bf1_at, (3, 0): late_col_at}

        def affines(d, y):
            zt = [placed([P, 2, P], F32, "zt%d_%d" % (d, h), zt_at[d, h]) if (d, h) in zt_at else kept([P, 2, P], F32, "zt%d_%d" % (d, h)) for h in range(2)]
            for c in range(2):
                nc.scalar.activation(zt[0][:, c, :], y[0][:, c, :], ACT.Identity, bias=calib_col[:, c, 1:2], scale=calib_col[:, c, 0:1])
            col = late_col[:] if d == 2 else calib_col[:, 2:4, :]
            for c in range(2):
                nc.vector.tensor_scalar(zt[1][:, c, :], y[1][:, c, :], col[:, c, 0:1], col[:, c, 1:2], ALU.mult, ALU.add)
            return zt

        def turn(d, zt, bank):
            z = psum.tile([P, S], F32, name="z%d" % d, tag="bank%d" % bank)
            for c in (0, 2, 1, 3) if d > 1 else range(CHUNKS):
                nc.tensor.transpose(z[:, c * P : (c + 1) * P], zt[c // 2][:, c % 2, :], ident[:])
            return z

        def row_max(d, z):
            neg_max = kept([P, 1], F32, "neg_max%d" % d)
            nc.vector.tensor_reduce(neg_max[:], z[:], AX.X, ALU.max, negate=True)
            return neg_max

        def exponential(d, z, neg_max):
            total = kept([P, 1], F32, "total%d" % d)
            e = kept([P, S], F32, "e%d" % d)
            nc.scalar.activation(e[:], z[:], ACT.Exp, bias=neg_max[:], scale=1.0, accum_out=total[:])
            return e, total

        def invert(d, total):
            inv = kept([P, 1], F32, "inv%d" % d)
            nc.vector.reciprocal(inv[:], total[:])
            return inv

        def finish(d, e, inv):
            prob = kept([P, S], F32, "prob%d" % d)
            if d < 1:
                nc.gpsimd.tensor_scalar(prob[:], e[:], inv[:], 0.0, ALU.mult, ALU.add)
            else:
                nc.vector.tensor_scalar(prob[:], e[:], inv[:], None, ALU.mult)
            nc.sync.dma_start(out[d * P : (d + 1) * P, :], prob[:])

        gather_scales(0)
        interleave(0, scalar_cast)
        quantize(0)
        gather_scales(1)
        nc.scalar.copy(calib_col[:], calib_ps[:, :, P - 2 : P])
        nc.scalar.copy(late_col[:], calib_ps[:, 2:4, P - 2 : P])
        interleave(1, scalar_cast)
        quantize(1)
        interleave(2, nc.vector.tensor_copy)
        y0 = products(0, [0, 1])
        y1 = products(1, [2, 3])
        zt0 = affines(0, y0)
        quantize(2)
        interleave(3, scalar_cast)
        zt1 = affines(1, y1)
        quantize(3)
        z0 = turn(0, zt0, 4)
        m0 = row_max(0, z0)
        zt2 = affines(2, products(2, [0, 1]))
        e0, total0 = exponential(0, z0, m0)
        z1 = turn(1, zt1, 5)
        m1 = row_max(1, z1)
        zt3 = affines(3, products(3, [2, 3]))
        finish(0, e0, invert(0, total0))
        e1, total1 = exponential(1, z1, m1)
        z2 = turn(2, zt2, 6)
        m2 = row_max(2, z2)
        inv1 = invert(1, total1)
        e2, total2 = exponential(2, z2, m2)
        z3 = turn(3, zt3, 7)
        m3 = row_max(3, z3)
        finish(1, e1, inv1)
        finish(2, e2, invert(2, total2))
        e3, total3 = exponential(3, z3, m3)
        finish(3, e3, invert(3, total3))
